import numpy as np, ml_dtypes
CORES = [23,119,17,113]
N = 4
BF = ml_dtypes.bfloat16
W, K, LP, CAP, PR = 4096, 4096, 2, 256, 6
XS = (1, 2, 3)
MP = K >> LP
def coefs(rng, lo, hi):
    o = np.argsort(rng.random((8, 16, 16)), axis=1)
    v = rng.integers(1, 4, (8, 16, 16)) * np.where(o == 0, 1, np.where(o == 1, -1, 2 * rng.integers(0, 2, (8, 16, 16)) - 1))
    return np.where(o < rng.integers(lo, hi + 1, (8, 1, 16)), v, 0)
def rays(rng, top, dens):
    v = np.floor(rng.random((N, 8, 16, W)) * (np.reshape(top, (1, 8, 1, 1)) + 1.0))
    return (v * (rng.random((N, 8, 16, W)) < dens)).astype(np.int64)
def plant(rng, nn, pz, order, full=False, odd=()):
    c = coefs(rng, 6, 10); x = rng.integers(0, 16, (N, 8, 16, W))
    P = np.argsort(rng.random((8, 16)), axis=1); M = rng.integers(0, 16, 8)
    if full: x[:, 1::2] = np.floor(np.exp2(7.9 * rng.random((N, 4, 16, W)))).astype(np.int64)
    for g in range(8):
        m = M[g]; a, b, e = P[g, :3]; w = int(rng.integers(1, 4))
        if full or g in odd:
            c[g] = 2 * np.sign(c[g]); c[g, e] = rng.choice(np.array([-3, -1, 1, 3]), 16); x[:, g, e] |= 1
        c[g, :, m] = 0; c[g, a, m] = w; c[g, b, m] = -w
        for r in range(N):
            sg = np.zeros(W, np.int64); sg[:int(nn[r, g])] = -1; sg[W - int(pz[r, g]):] = 1
            if order[g] == 0: sg = rng.permutation(sg)
            if order[g] == 2: sg = sg[::-1]
            lo = rng.integers(0, 8, W); d = rng.integers(1, 8, W)
            if full: d = np.where(sg > 0, 7, 1)
            x[r, g, a] = lo + np.where(sg > 0, d, 0); x[r, g, b] = lo + np.where(sg < 0, d, 0)
    return x, c, P, M
def pack(x, c):
    return {"x": np.ascontiguousarray(x.reshape(N, 128, W)).astype(np.float32).astype(BF), "q": np.stack([c.reshape(128, 16)] * N).astype(np.int32)}
def setup_inputs(rng):
    top = rng.permutation(np.array([15, 15, 40, 40, 100, 100, 255, 255]))
    return pack(rays(rng, top, rng.choice(np.array([0.1, 0.3, 0.6, 1.0]), (N, 8, 16, 1))), coefs(rng, 2, 6))
def setup_inputs_room(rng):
    nn = rng.choice(np.array([0, 1, CAP - 1, CAP, CAP + 1, 2 * CAP]), (N, 8)); pz = rng.choice(np.array([0, 1, MP - 1, MP, MP + 1]), (N, 8))
    nn[0] = (CAP, CAP + 1, CAP - 1, CAP, 1, 0, 2 * CAP, CAP + 1); pz[0] = (MP, MP + 1, MP - 1, 1, MP, MP + 1, MP, 0)
    nn[XS[0]] = (2 * CAP, CAP, CAP + 1, CAP - 1, CAP, CAP, 1, CAP); pz[XS[0]] = (MP + 1, MP, MP, MP - 1, MP, MP + 1, MP, MP)
    x, c, P, M = plant(rng, nn, pz, np.zeros(8, np.int64))
    return pack(x, c)
def setup_inputs_full(rng):
    few = CAP + rng.integers(0, 64, (N, 8)); many = W - MP - rng.integers(72, 136, (N, 8))
    nn = np.where(np.array([0, 1, 1, 0, 0, 1, 1, 0]) == 1, many, few); pz = MP + rng.integers(0, 64, (N, 8))
    o = XS[0]; p = W // (2 ** LP + 1)
    nn[0, 0] = CAP; nn[o, 3] = CAP; pz[0, :2] = MP; nn[0, 2] = W - p; pz[0, 2] = p
    x, c, P, M = plant(rng, nn, pz, np.array([0, 0, 0, 0, 1, 1, 2, 2]), True)
    a, b, e, f0, f1, f2, f3 = P[2, :7]
    up = x[0, 2, a] > x[0, 2, b]; dn = x[o, 2, a] < x[o, 2, b]
    x[0, 2, a] = np.where(up, rng.integers(1, 16, W), 0); x[0, 2, b] = np.where(up, 0, rng.integers(2, 8, W))
    u = np.zeros(W, np.int64); u[up] = rng.permutation(4096)[:p]
    for k, v in ((f0, u >> 6), (f1, 63 - (u >> 6)), (f2, u & 63), (f3, 63 - (u & 63))):
        x[0, 2, k] = np.where(up, v, x[0, 2, k]); x[o, 2, k] = np.where(dn, 0, x[o, 2, k])
    x[o, 2, a] = np.where(dn, 0, x[o, 2, a]); x[o, 2, b] = np.where(dn, 1, x[o, 2, b])
    return pack(x, c)
def setup_inputs_ties(rng):
    c = coefs(rng, 2, 4); c[:, :, 8:] = -c[:, :, rng.permutation(8)]; c[0, :, 15] = 0; c[4, :, 0] = 0
    x = rays(rng, np.array([1, 1, 2, 2, 3, 1, 2, 15]), rng.choice(np.array([0.4, 0.6, 0.9]), (N, 8, 16, 1)))
    h = W // 2
    for g in (2, 5): x[:, g, :, h:] = x[:, g][:, :, rng.permutation(h)]
    x[:, 7] = 255 * (rng.random((N, 16, W)) < 0.4)
    return pack(x, c)
def setup_inputs_lean(rng):
    h = W // 2; nn = rng.integers(h // 4, h // 2, (N, 8)); pz = rng.integers(h // 4, h // 2, (N, 8)); o = XS[0]
    nn[:, 0] = 0; pz[:, 1] = 0
    nn[0, 2] = W; pz[0, 2] = 0; nn[o, 2] = h; pz[o, 2] = W - h
    nn[0, 3] = 0; pz[0, 3] = 0; nn[o, 3] = 0; pz[o, 3] = W
    nn[0, 6] = 1; pz[0, 6] = W - 1
    for r in (0, XS[1], XS[0] ^ XS[1]): nn[r, 4] = h // 2; pz[r, 4] = h // 16
    nn[o, 4] = 16; pz[o, 4] = h // 2
    x, c, P, M = plant(rng, nn, pz, np.array([0, 0, 0, 0, 1, 2, 1, 2]), False, (0, 1, 4))
    a, b, e, k, l = P[0, :5]; m = M[0]
    c[0][:, [0, m]] = c[0][:, [m, 0]]; c[0, b, 0] = 0; x[:, 0, a] -= x[:, 0, b]
    c[0, :, 1] = 0; c[0, e, 1] = 2 * rng.integers(0, 2) - 1; c[0, k, 1] = 2; c[0, l, 1] = -2
    a, b = P[1, :2]; c[1, a, M[1]] = 0; x[:, 1, b] -= x[:, 1, a]
    c[4, :, (M[4] + rng.integers(1, 16)) % 16] = c[4, :, M[4]]
    return pack(x, c)
def setup_inputs_spread(rng):
    u = rng.random((N, 8, 16, W)); u[:, 6] = 0.5 + 0.5 * u[:, 6]
    v = np.floor(np.exp2(3 + 5 * rng.random((N, 8, 1, W))) * u) * (rng.random((N, 8, 1, W)) > 0.0625)
    kept = rng.random((N, 8, 16, W)) < rng.choice(np.array([0.4, 0.7, 1.0]), (N, 8, 16, 1)); kept[:, 6] = True
    v = np.minimum(v * kept, 255).astype(np.int64); c = coefs(rng, 2, 16)
    up = rng.permutation(16) < 8; side = (rng.random((N, 1, W)) < 0.5) == up[None, :, None]
    v[:, 7] = np.where(side, rng.integers(192, 256, (N, 16, W)), rng.integers(0, 32, (N, 16, W)))
    c[7] = np.where(up[:, None], 1, -1) * rng.choice(np.array([2, 3, 3, 3]), (16, 16)) * rng.choice(np.array([-1, 1]), (1, 16))
    return pack(v, c)
def check_inputs(d):
    bad = []; x = np.asarray(d["x"]).astype(np.float32); q = np.asarray(d["q"])
    if not (np.all(x >= 0) and np.all(x <= 255) and np.all(x == np.floor(x))): bad.append("range of x")
    if np.min(q) < -3 or np.max(q) > 3: bad.append("range of q")
    if not np.all(q == q[:1]): bad.append("q alike on all ranks")
    return bad
def reference(x, q):
    cur = np.ascontiguousarray(x.astype(np.float32).reshape(N, 8, 16, W).transpose(0, 1, 3, 2)).astype(np.int16)
    co = q[0].astype(np.float32).reshape(8, 16, 16)
    used = np.zeros((8, 16), bool)
    k = np.arange(K); i = k >> LP
    for t in range(len(XS)):
        val = np.matmul(cur.astype(np.float32), co[None])
        cnt = np.where(used, N * W + 1, np.count_nonzero(val, axis=(0, 2)))
        m = np.argmin(cnt, axis=1)
        used[np.arange(8), m] = True
        s = np.take_along_axis(val, m[None, :, None, None], 3)[..., 0].astype(np.int64)
        j = (37 * i + (CAP >> LP) * (k & (2 ** LP - 1)) + t) & (CAP - 1)
        new = cur.copy()
        for r in range(N):
            o = r ^ XS[t]
            for g in range(8):
                own = cur[r, g]; neg = np.flatnonzero(s[r, g] < 0); pos = np.flatnonzero(s[r, g] > 0); guest = np.flatnonzero(s[o, g] < 0)[:CAP]
                ks = np.flatnonzero((i < len(pos)) & (j < len(guest)))
                a = pos[i[ks]]; b = guest[j[ks]]; keep = s[r, g, a] + s[o, g, b] >= 0
                a = a[keep]; b = b[keep]
                z = np.minimum(own[a] + cur[o, g][b], 255)
                v = (17 * a + 5 * j[ks][keep]) & (W - 1); alive = np.ones(len(a), bool)
                for n in range(PR):
                    c = np.where(v == a, 16, np.count_nonzero(own[v] > z, axis=1))
                    alive = alive & (c > 0)
                    v = (5 * v + 241 * c + 1) & (W - 1)
                z = z[alive]; h = min(len(z), len(neg))
                new[r, g, neg[:h]] = z[:h]
        cur = new
    return {"y": np.ascontiguousarray(cur.transpose(0, 1, 3, 2)).reshape(N, 128, W).astype(np.float32).astype(BF)}

@@ -1,0 +1,635 @@
+import numpy as np
+from concourse.bass import DstId, RemoteDMATransfer
+from concourse.mybir import dt, AluOpType as A, AxisListType, ActivationFunctionType as F
+
+SV, SA, XO, XE, BWC = 2048, 4096, 6144, 10240, 10272
+SB = {
+    "BW0": (BWC, "bfloat16"), "BW1": (BWC, "bfloat16"), "SAf": (4096, "float32"), "Zp": (4096, "bfloat16"),
+    "Zf": (2048, "float32"), "Pg": (1024, "bfloat16"), "Hs": (256, "bfloat16"), "Hl": (256, "bfloat16"),
+    "c1n": (256, "bfloat16"), "c2n": (256, "bfloat16"), "c3n": (256, "bfloat16"),
+    "c1p": (1024, "bfloat16"), "c2p": (1024, "bfloat16"), "c3p": (1024, "bfloat16"),
+    "cmp": (4096, "bfloat16"), "G": (2048, "bfloat16"), "acc": (8, "float32"),
+    "cown0": (1, "float32"), "cown1": (1, "float32"), "cown2": (1, "float32"),
+    "cl0": (4, "float32"), "cl1": (4, "float32"), "cl2": (4, "float32"),
+    "qi": (16, "int32"), "qf": (16, "float32"), "Qblk": (128, "bfloat16"), "kap16": (1, "float32"),
+    "pi": (1, "int32"), "p16i": (1, "int32"), "pgi": (1, "int32"), "pif": (1, "float32"), "p16f": (1, "float32"),
+    "pgf": (1, "float32"), "e15": (1, "float32"), "p37": (1, "float32"), "ci": (144, "int32"), "cg": (128, "int32"),
+    "Bones": (128, "bfloat16"), "BonesF": (128, "float32"), "ident": (128, "bfloat16"), "identF": (128, "float32"),
+    "nident": (128, "bfloat16"), "I3856": (128, "bfloat16"), "I1928": (128, "bfloat16"), "I16384": (128, "bfloat16"),
+    "N16384": (128, "bfloat16"), "EM1": (144, "bfloat16"), "EM16": (144, "bfloat16"), "EM256": (144, "bfloat16"),
+    "EM241": (144, "bfloat16"), "EM120": (144, "bfloat16"), "E": (144, "bfloat16"), "M16f": (16, "float32"),
+    "mask16": (16, "float32"), "base": (16, "float32"), "obig": (16, "float32"), "rown": (16, "float32"),
+    "rpeer": (16, "float32"), "Dm": (128, "bfloat16"), "Ds": (128, "bfloat16"), "dtmp": (128, "bfloat16"),
+    "B255": (128, "bfloat16"), "col255": (1, "bfloat16"), "Ji": (602, "int32"), "Jm": (602, "int32"), "JF": (602, "float32"),
+    "IF": (1024, "float32"), "IU": (1024, "uint16"), "JTi": (384, "int32"), "JTk": (384, "int32"), "JTm": (384, "int32"),
+    "JT": (384, "float32"), "VTi": (256, "int32"), "VT": (256, "float32"), "KT": (128, "float32"),
+    "onesF": (256, "float32"), "onesB": (64, "bfloat16"), "W2": (48, "float32"), "W3": (528, "float32"),
+    "t3": (1, "float32"), "mn": (1, "float32"), "oh": (16, "float32"), "cq": (16, "float32"), "csel": (1, "float32"),
+    "csb": (1, "bfloat16"), "kaps": (1, "float32"), "kap2": (1, "float32"), "Fl": (512, "bfloat16"), "T2b": (32, "bfloat16"),
+    "I3": (512, "float32"), "I2": (32, "float32"), "bt": (32, "float32"), "bnd": (8, "float32"),
+    "oAn": (16, "uint16"), "oQn": (16, "uint16"), "oPn": (16, "uint16"), "oAp": (64, "uint16"), "oQp": (64, "uint16"),
+    "oPp": (64, "uint16"), "A17": (64, "float32"),
+    "t32": (256, "int32"), "vi": (256, "int32"), "off": (256, "uint16"), "Tf5": (256, "float32"), "eq": (256, "bfloat16"),
+    "NZ": (1792, "bfloat16"), "shr": (48, "float32"), "AL": (256, "bfloat16"), "sc": (64, "float32"), "pb": (64, "float32"),
+    "of": (256, "float32"), "mx": (256, "float32"), "so": (256, "uint16"), "nS": (1, "float32"), "dA": (1, "float32"),
+    "g1": (256, "float32"), "g2": (256, "float32"), "fo": (256, "float32"), "fo16": (256, "uint16"),
+}
+SCRATCH = {n: ("sbuf", [128, -(-c // 16) * 16], d) for n, (c, d) in SB.items()}
+for _b in range(8):
+    SCRATCH["b%d" % _b] = ("psum", [128, 512], "float32")
+NX = 8
+QSEM = {"tensor": "sT", "vector": "sV", "scalar": "sS", "g": "sG"}
+SEMAPHORES = (["sT", "sV", "sS", "sG", "qld"] + ["xl%d" % i for i in range(NX)] + ["ys%d" % i for i in range(8)]
+              + ["%s%d" % (s, t) for s in ("cs", "gs", "lc", "lg") for t in range(3)])
+XS = (1, 2, 3)
+BIG = 1048576.0
+MAGIC = 8388608.0
+CE = 4
+
+
+def make_queue(g, T):
+    ops, hist = [], {}
+    eng = {"tensor": g.tensor, "vector": g.vector, "scalar": g.scalar, "sync": g.sync, "g": g}
+
+    def op(q, fn, reads, writes, sem=None, val=0):
+        me = len(ops)
+        rec = {"q": q, "fn": fn, "deps": set(), "sem": sem, "val": val, "need": False, "m": []}
+        acc = []
+        for w in writes:
+            if w[0] == "IND":
+                acc += [(w[1], True), (w[2], False)]
+            else:
+                acc.append((w, True))
+        for r in reads:
+            if r[0] == "IND":
+                acc += [(r[1], False), (r[2], False)]
+            else:
+                acc.append((r, False))
+
+        def mine(o):
+            return o["q"] == q and o["sem"] is None
+        for (n, a, b, _ap), isw in acc:
+            ps = n[0] == "b" and len(n) == 2
+            for (oa, ob, o, ow) in hist.setdefault(n, []):
+                if o == me:
+                    continue
+                hit = oa < b and a < ob
+                if mine(ops[o]):
+                    need = hit and ow and not (ps and q == "tensor")
+                else:
+                    need = ps or (hit and (ow or isw))
+                if need:
+                    rec["deps"].add(o)
+        ops.append(rec)
+        for (n, a, b, _ap), isw in acc:
+            ps = n[0] == "b" and len(n) == 2
+            keep = []
+            for e in hist[n]:
+                inside = a <= e[0] and e[1] <= b
+                if e[2] != me and ((inside and isw) or (inside and not e[3] and mine(ops[e[2]]))
+                                   or (ps and not mine(ops[e[2]]) and not e[3])):
+                    continue
+                keep.append(e)
+            keep.append((a, b, me, isw))
+            hist[n] = keep
+
+    def emit():
+        for r in ops:
+            for d in r["deps"]:
+                ops[d]["need"] = True
+        cnt = {q: 0 for q in QSEM}
+        know = {q: {} for q in eng}
+        for r in ops:
+            q = r["q"]
+            if q is None:
+                r["clock"] = {r["sem"]: r["val"], "own": r["sem"]}
+                continue
+            k = know[q]
+            todo = {}
+            for d in sorted(r["deps"], reverse=True):
+                o = ops[d]
+                s, v = (o["sem"], o["val"]) if o["sem"] is not None else (QSEM[o["q"]], o["at"])
+                if k.get(s, 0) < v and todo.get(s, 0) < v:
+                    todo[s] = v
+                    r["m"].append(o["clock"])
+            for s in sorted(todo):
+                if not any(c["own"] != s and c.get(s, 0) >= todo[s] for c in r["m"]):
+                    eng[q].wait_ge(T.sem[s], int(todo[s]))
+            for c in r["m"]:
+                for s, v in c.items():
+                    if s != "own" and k.get(s, 0) < v:
+                        k[s] = v
+            ins = r["fn"]()
+            if r["sem"] is not None:
+                c = dict(k)
+                c[r["sem"]] = r["val"]
+                c["own"] = r["sem"]
+                if q != "g":
+                    ins.then_inc(T.sem[r["sem"]], r["val"])
+            else:
+                s = QSEM[q]
+                c = dict(k)
+                c["own"] = s
+                if r["need"]:
+                    cnt[q] += 1
+                    ins.then_inc(T.sem[s], 1)
+                    c[s] = cnt[q]
+                    r["at"] = cnt[q]
+            r["clock"] = c
+        for q, n in cnt.items():
+            if n:
+                g.wait_ge(T.sem[QSEM[q]], n)
+        for r in ops:
+            if r["sem"] is not None and r["sem"][:2] in ("ys", "lc", "lg"):
+                g.wait_ge(T.sem[r["sem"]], r["val"])
+
+    return op, emit
+
+
+def rank_program(g, core, T, topo):
+    rank = T.rank_of(core)
+    if rank is None:
+        return
+    op, emit = make_queue(g, T)
+
+    def S(n, a=0, b=None, st=1):
+        if b is None:
+            b = SB[n][0] if n in SB else 512
+        return (n, a, b, T[n][:, a:b] if st == 1 else T[n][:, a:b:st])
+
+    def IND(w, o):
+        return ("IND", w, o)
+
+    def AP(x):
+        return x[1][3].indirect(x[2][3]) if x[0] == "IND" else x[3]
+
+    def num(x):
+        return isinstance(x, (int, float))
+
+    def cp(out, in_):
+        op("vector", lambda: g.vector.tensor_copy(AP(out), AP(in_)), [in_], [out])
+
+    def tt(out, a, b, o):
+        op("vector", lambda: g.vector.tensor_tensor(AP(out), AP(a), AP(b), o), [a, b], [out])
+
+    def ts(out, a, s1, o0, s2=None, o1=None):
+        cols = [x for x in (s1, s2) if x is not None and not num(x)]
+        u1 = s1 if num(s1) else AP(s1)
+        if o1 is None:
+            op("vector", lambda: g.vector.tensor_scalar(AP(out), AP(a), u1, None, o0), [a] + cols, [out])
+        else:
+            u2 = s2 if num(s2) else AP(s2)
+            op("vector", lambda: g.vector.tensor_scalar(AP(out), AP(a), u1, u2, o0, o1), [a] + cols, [out])
+
+    def red(out, a, o):
+        op("vector", lambda: g.vector.tensor_reduce(AP(out), AP(a), AxisListType.X, o), [a], [out])
+
+    def scan(out, a, n):
+        one = S("onesF", 0, n)
+        op("vector", lambda: g.vector.tensor_tensor_scan(AP(out), AP(one), AP(a), 0.0, A.mult, A.add), [one, a], [out])
+
+    def fill(out, c):
+        op("vector", lambda: g.vector.memset(AP(out), c), [], [out])
+
+    def act(out, a, f, bias=0.0, scale=1.0, accum=None):
+        if accum is None:
+            if f == F.Silu:
+                op("scalar", lambda: g.scalar.activation(AP(out), AP(a), f), [a], [out])
+            else:
+                op("scalar", lambda: g.scalar.activation(AP(out), AP(a), f, bias=bias, scale=scale), [a], [out])
+        else:
+            op("scalar", lambda: g.scalar.activation(AP(out), AP(a), f, accum_out=AP(accum)), [a], [out, accum])
+
+    def mm(out, l, r, start, stop):
+        op("tensor", lambda: g.tensor.matmul(AP(out), AP(l), AP(r), start, stop), [l, r], [out])
+
+    def spread(bank, c0, n, emat, src, s0, start, stop):
+        for p in range(16):
+            mm(S(bank, c0, c0 + n), S(emat, 15 - p, 143 - p), S(src, s0 + p, s0 + 16 * n, 16), start and p == 0, stop and p == 15)
+
+    def iota(out, pattern, base=0, cm=0, fl=False):
+        if fl:
+            op("g", lambda: g.iota(AP(out), pattern, base, cm, allow_small_or_imprecise_dtypes=True), [], [out])
+        else:
+            op("g", lambda: g.iota(AP(out), pattern, base, cm), [], [out])
+
+    op("sync", lambda: g.sync.dma_start(T.qi[:, 0:16], T.q[:]), [], [S("qi")], "qld", 16)
+    w = 4096 // NX
+
+    def load(i, q):
+        o = S("BW1", XO + w * i, XO + w * i + w)
+        op(q, lambda: (g.sync if q == "sync" else g.scalar).dma_start(AP(o), T.x[:, w * i:w * i + w]), [], [o], "xl%d" % i, 16)
+    for i in range(NX):
+        load(i, "sync" if i % 2 else "scalar")
+    iota(S("pi"), [[1, 1]], 0, 1)
+    iota(S("ci"), [[1, 144]])
+    iota(S("Ji"), [[37, 602]])
+    iota(S("IF"), [[1, 1024]], 0, 0, True)
+    iota(S("JTi"), [[1, 3], [64, 4], [592, 32]])
+    iota(S("VTi"), [[16, 256]], 4096)
+    ts(S("p16i"), S("pi"), 15, A.bitwise_and)
+    ts(S("pgi"), S("pi"), 4, A.arith_shift_right)
+    cp(S("pif"), S("pi"))
+    ts(S("cg"), S("ci", 0, 128), 4, A.arith_shift_right)
+    cp(S("pgf"), S("pgi"))
+    cp(S("p16f"), S("p16i"))
+    ts(S("BonesF"), S("cg"), S("pgf"), A.is_equal)
+    ts(S("M16f"), S("ci", 0, 16), S("p16f"), A.is_equal, 16.0, A.mult)
+    ts(S("identF"), S("ci", 0, 128), S("pif"), A.is_equal)
+    cp(S("base"), S("ci", 0, 16))
+    tt(S("e15"), S("pif"), S("p16f"), A.subtract)
+    for k in range(8):
+        ts(S("Qblk", 16 * k, 16 * k + 16), S("qi"), S("BonesF", 16 * k, 16 * k + 1), A.mult)
+
+    def consts_a():
+        ts(S("e15"), S("e15"), 15.0, A.add)
+        cp(S("qf"), S("qi"))
+        ts(S("dtmp"), S("ci", 0, 128), S("pif"), A.is_lt, -1.0, A.mult)
+        ts(S("EM1"), S("ci"), S("e15"), A.is_equal)
+        act(S("Bones"), S("BonesF"), F.Copy)
+        act(S("B255"), S("BonesF"), F.Copy, scale=255.0)
+        act(S("ident"), S("identF"), F.Copy)
+        tt(S("Dm"), S("dtmp"), S("BonesF"), A.mult)
+        for n, s in (("EM16", 16.0), ("EM256", 256.0)):
+            act(S(n), S("EM1"), F.Copy, scale=s)
+        for b in range(8):
+            o, i = S("BW0", XO + 512 * b, XO + 512 * b + 512), S("BW1", XO + 512 * b, XO + 512 * b + 512)
+            if b in (2, 5, 7):
+                act(o, i, F.Identity, bias=255.0, scale=-1.0)
+            else:
+                ts(o, i, -1.0, A.mult, 255.0, A.add)
+        fill(S("BW0", XE, BWC), 0.0)
+        fill(S("BW1", XE, BWC), 0.0)
+        ts(S("mask16"), S("M16f"), 0.0625, A.mult)
+        fill(S("onesF"), 1.0)
+        for a, b in ((16, 24), (40, 48)):
+            fill(S("W2", a, b), 1000000.0)
+        for a, b in ((256, 264), (520, 528)):
+            fill(S("W3", a, b), 1000000.0)
+
+    def consts_b():
+        for n, s in (("EM241", 241.0), ("EM120", 120.5)):
+            act(S(n), S("EM1"), F.Copy, scale=s)
+        for n, s in (("nident", -1.0), ("I3856", 3856.0), ("I1928", 1928.0), ("I16384", 16384.0), ("N16384", -16384.0)):
+            act(S(n), S("identF"), F.Copy, scale=s)
+        act(S("SAf", 2048, 4096), S("BW1", XO, XO + 2048), F.Copy)
+        act(S("BW0", SV, SA), S("BW1", XO, XO + 2048), F.Copy)
+        ts(S("Jm"), S("Ji"), 255, A.bitwise_and)
+        ts(S("p37"), S("p16f"), 37.0, A.mult)
+        cp(S("JF"), S("Jm"))
+
+    def consts_c():
+        ts(S("JTk"), S("JTi"), S("p37"), A.add)
+        fill(S("col255"), 255.0)
+        tt(S("Ds"), S("Dm"), S("identF"), A.subtract)
+        ts(S("JTm"), S("JTk"), 255, A.bitwise_and)
+        fill(S("onesB"), 1.0)
+        ts(S("VT"), S("VTi"), S("p16f"), A.add, -16383.0, A.add)
+        ts(S("JT"), S("JTm"), 5.0, A.mult)
+        ts(S("KT"), S("VT", 0, 128), 26623.0, A.add)
+        mm(S("b2", 0, 1), S("Qblk"), S("col255"), True, True)
+        cp(S("kap16"), S("b2", 0, 1))
+
+    def consts_d():
+        cp(S("IU"), S("IF"))
+        act(S("BW1", SV, SA), S("BW0", XO, XO + 2048), F.Copy)
+
+    peers = [r for r in range(len(T.cores)) if r != rank]
+    peers.sort(key=lambda r: len(topo.engines(core, T.cores[r])))
+    used, plan = [], []
+    for r in peers:
+        es = [e for e in topo.engines(core, T.cores[r]) if e not in used][:CE]
+        used += es
+        plan.append((r, sum(1 << e for e in es)))
+
+    def send_counts(t):
+        def f():
+            tr = []
+            for r, m in plan:
+                rid, pid, _s = topo.addr(T.cores[r])
+                c = [k for k in range(len(T.cores)) if k != r].index(rank)
+                tr.append(RemoteDMATransfer(dst_ids=[DstId(rid=rid, pnc=pid)], dma_engine_mask=m, remote_sem=T.sem["cs%d" % t],
+                                            src=T["cown%d" % t][:, 0:1], dst=T["cl%d" % t][:, c:c + 1]))
+            return g.remote_dma_fused(tr, local_sem=T.sem["lc%d" % t])
+        op("g", f, [S("cown%d" % t)], [], "lc%d" % t, CE * len(peers))
+        op(None, None, [], [S("cl%d" % t)], "cs%d" % t, CE * len(peers))
+
+    def send_guests(t):
+        dst = T.cores[rank ^ XS[t]]
+        es = topo.engines(core, dst)[:8]
+
+        def f():
+            rid, pid, _s = topo.addr(dst)
+            return g.remote_dma(T.Hl[:, 0:256], T.Hs[:, 0:256], T.sem["gs%d" % t], T.sem["lg%d" % t], pid, rid, sum(1 << e for e in es))
+        op("g", f, [S("Hs")], [], "lg%d" % t, len(es))
+
+    def guests_come(t):
+        src = T.cores[rank ^ XS[t]]
+        op(None, None, [], [S("Hl")], "gs%d" % t, len(topo.engines(src, core)[:8]))
+
+    for t in range(3):
+        cur, nxt = ("BW0", "BW1") if t % 2 == 0 else ("BW1", "BW0")
+        xs = "BW1" if t == 0 else cur
+        X = S(cur, XO, BWC)
+        for b in range(8):
+            sl = (512 * b, 512 * b + 512)
+            mm(S("b%d" % b), S("Qblk"), S(xs, XO + sl[0], XO + sl[1]), True, True)
+            ts(S("cmp", *sl), S("b%d" % b), 0.0 if t == 0 else S("kap16"), A.not_equal)
+            act(S("G", 512 * (b % 4), 512 * (b % 4) + 512), S("cmp", *sl), F.Copy, accum=S("acc", b, b + 1))
+        cown, cl = S("cown%d" % t), S("cl%d" % t, 0, 3)
+        red(cown, S("acc"), A.add)
+        send_counts(t)
+        ts(S("rown"), S("M16f"), cown, A.mult)
+        mm(S("b0", 0, 16), S("identF"), S("base"), True, False)
+        mm(S("b0", 0, 16), S("BonesF"), S("rown"), False, False)
+        if t == 0:
+            consts_a()
+        if t == 1:
+            consts_d()
+        red(S("t3"), cl, A.add)
+        ts(S("rpeer"), S("M16f"), S("t3"), A.mult)
+        mm(S("b0", 0, 16), S("BonesF"), S("rpeer"), False, True)
+        red(S("mn"), S("b0", 0, 16), A.min)
+        ts(S("oh"), S("b0", 0, 16), S("mn"), A.is_equal)
+        tt(S("cq"), S("oh"), S("qf"), A.mult)
+        red(S("csel"), S("cq"), A.add)
+        ts(S("E"), S("EM1"), S("csel"), A.mult)
+        cp(S("csb"), S("csel"))
+        mm(S("b1", 0, 1), S("B255"), S("csb"), True, True)
+        spread("b2", 0, 256, "E", cur, XO, True, True)
+        cp(S("kaps"), S("b1", 0, 1))
+        ts(S("obig"), S("oh"), BIG, A.mult)
+        ts(S("kap2"), S("kaps"), 2.0, A.mult)
+        tt(S("base"), S("base"), S("obig"), A.add)
+        if t == 0:
+            consts_b()
+        ts(S("Fl", 0, 256), S("b2", 0, 256), S("kaps"), A.is_gt)
+        ts(S("Fl", 256, 512), S("b2", 0, 256), S("kaps"), A.is_lt)
+        for p in range(16):
+            mm(S("b3", 0, 32), S("EM1", 15 - p, 143 - p), S("Fl", p, 512, 16), p == 0, p == 15)
+        mm(S("b4"), S("Bones"), S("Fl"), True, True)
+        mm(S("b5"), S("Dm"), S("Fl"), True, True)
+        cp(S("T2b"), S("b3", 0, 32))
+        mm(S("b6", 0, 32), S("Bones"), S("T2b"), True, True)
+        mm(S("b6", 32, 64), S("Dm"), S("T2b"), True, True)
+        scan(S("I3", 0, 256), S("b4", 0, 256), 256)
+        scan(S("I2", 0, 16), S("b6", 0, 16), 16)
+        scan(S("I2", 16, 32), S("b6", 16, 32), 16)
+        tt(S("bt", 0, 16), S("I2", 0, 16), S("mask16"), A.mult)
+        tt(S("bt", 16, 32), S("I2", 16, 32), S("mask16"), A.mult)
+        red(S("bnd", 0, 1), S("bt", 0, 16), A.add)
+        red(S("bnd", 4, 5), S("bt", 16, 32), A.add)
+        J = S("JF", 173 * t, 173 * t + 256)
+        ts(S("c1n"), J, S("bnd", 0, 1), A.is_ge)
+        spread("b7", 0, 16, "EM1", "c1n", 0, True, True)
+        spread("b0", 0, 16, "EM16", "c1n", 0, True, False)
+        tt(S("W2", 0, 16), S("I2", 0, 16), S("b6", 32, 48), A.add)
+        tt(S("W2", 24, 40), S("I2", 16, 32), S("b6", 48, 64), A.add)
+        tt(S("W3", 0, 256), S("I3", 0, 256), S("b5", 0, 256), A.add)
+        cp(S("oAn"), S("b7", 0, 16))
+        tt(S("c2n"), IND(S("W2", 0, 24), S("oAn")), J, A.is_le)
+        spread("b0", 0, 16, "EM1", "c2n", 0, False, True)
+        spread("b3", 0, 16, "EM256", "c1n", 0, True, False)
+        spread("b3", 0, 16, "EM16", "c2n", 0, False, False)
+        ts(S("c1p"), S("IF" if t == 0 else "IU"), S("bnd", 4, 5), A.is_ge)
+        cp(S("oQn"), S("b0", 0, 16))
+        tt(S("c3n"), IND(S("W3", 0, 264), S("oQn")), J, A.is_le)
+        spread("b3", 0, 16, "EM1", "c3n", 0, False, True)
+        spread("b1", 0, 64, "EM1", "c1p", 0, True, True)
+        spread("b6", 0, 64, "EM16", "c1p", 0, True, False)
+        scan(S("I3", 256, 512), S("b4", 256, 512), 256)
+        cp(S("oPn"), S("b3", 0, 16))
+        act(S("Hs"), IND(X, S("oPn")), F.Copy)
+        send_guests(t)
+        cp(S("oAp"), S("b1", 0, 64))
+        tt(S("c2p"), IND(S("W2", 24, 48), S("oAp")), S("IF"), A.is_le)
+        spread("b6", 0, 64, "EM1", "c2p", 0, False, True)
+        spread("b7", 0, 64, "EM256", "c1p", 0, True, False)
+        tt(S("W3", 264, 520), S("I3", 256, 512), S("b5", 256, 512), A.add)
+        spread("b7", 0, 64, "EM16", "c2p", 0, False, False)
+        if t == 0:
+            consts_c()
+        cp(S("oQp"), S("b6", 0, 64))
+        tt(S("c3p"), IND(S("W3", 264, 528), S("oQp")), S("IF"), A.is_le)
+        spread("b7", 0, 64, "EM1", "c3p", 0, False, True)
+        cp(S("oPp"), S("b7", 0, 64))
+        ts(S("A17"), S("b7", 0, 64), 17.0, A.mult)
+        for hf in range(2):
+            act(S("Pg", 512 * hf, 512 * hf + 512), IND(X, S("oPp", 32 * hf, 32 * hf + 32)), F.Copy)
+        for hf in (0, 1):
+            for ww in range(4):
+                o = 128 * hf + 32 * ww
+                tt(S("t32", o, o + 32), S("A17", 32 * hf, 32 * hf + 32), S("JT", 128 * t + 32 * ww, 128 * t + 32 * ww + 32), A.add)
+            h = (128 * hf, 128 * hf + 128)
+            ts(S("vi", *h), S("t32", *h), 4095, A.bitwise_and)
+            cp(S("off", *h), S("vi", *h))
+        for c in range(4):
+            for k in range(2):
+                act(S("b%d" % c, 128 + 32 * k, 160 + 32 * k), S("b7", 32 * (c // 2), 32 * (c // 2) + 32), F.Copy)
+
+        def gather_s(c):
+            act(S("G", 1024 * (c - 2), 1024 * (c - 2) + 1024), IND(X, S("off", 64 * c, 64 * c + 64)), F.Copy)
+
+        def equal(c):
+            h = (64 * c, 64 * c + 64)
+            ts(S("Tf5", *h), S("vi", *h), 5.0, A.mult, 1.0, A.add)
+            tt(S("eq", *h), S("vi", *h), S("b%d" % c, 128, 192), A.is_equal)
+        gather_s(2)
+        gather_s(3)
+        guests_come(t)
+        ub = {0: 4, 1: 6, 2: 6, 3: 4}
+
+        def sums(c):
+            for k in range(2):
+                ww = 2 * (c % 2) + k
+                b = "b%d" % (ub[c] + k)
+                mm(S(b), S("ident"), S("Pg", 512 * (c // 2), 512 * (c // 2) + 512), True, False)
+                for o in (0, 256):
+                    mm(S(b, o, o + 256 - 64 * ww), S("ident"), S("Hl", 64 * ww, 256), False, o == 256 and ww == 0)
+                    if ww:
+                        mm(S(b, o + 256 - 64 * ww, o + 256), S("ident"), S("Hl", 0, 64 * ww), False, o == 256)
+
+        def children(c):
+            for k in range(2):
+                b = S("b%d" % (ub[c] + k))
+                o = S("Zp", 1024 * c + 512 * k, 1024 * c + 512 * k + 512)
+                if c == 3:
+                    act(o, b, F.Relu, bias=-255.0)
+                else:
+                    ts(o, b, -255.0, A.add, 0.0, A.max)
+
+        def diff(c):
+            for k in range(2):
+                b = "b%d" % (2 * c + k)
+                o = 1024 * (c - 2) + 512 * k
+                mm(S(b), S("ident"), S("Zp", 1024 * c + 512 * k, 1024 * c + 512 * k + 512), True, False)
+                mm(S(b), S("nident"), S("G", o, o + 512), False, True)
+
+        def sign(c):
+            for k in range(2):
+                o = 1024 * c + 512 * k
+                act(S("cmp", o, o + 512), S("b%d" % (2 * c + k)), F.Sign, bias=-0.5)
+
+        def compare(c):
+            tt(S("cmp", 1024 * c, 1024 * c + 1024), IND(X, S("off", 64 * c, 64 * c + 64)), S("Zp", 1024 * c, 1024 * c + 1024), A.is_lt)
+
+        def total(c):
+            b = "b%d" % c
+            h = (64 * c, 64 * c + 64)
+            mm(S(b, 0, 64), S("identF"), S("Tf5", *h), True, False)
+            mm(S(b, 0, 64), S("I3856"), S("eq", *h), False, False)
+            if c >= 2:
+                mm(S(b, 0, 64), S("I1928"), S("onesB"), False, False)
+            spread(b, 0, 64, "EM241" if c < 2 else "EM120", "cmp", 1024 * c, False, True)
+
+        late = []
+
+        def flush():
+            while late:
+                equal(late.pop())
+
+        def update(c, n):
+            b = S("b%d" % c, 0, 64)
+            h = (64 * c, 64 * c + 64)
+            if n < 5:
+                cp(S("t32", *h), b)
+            tt(S("NZ", 256 * n + h[0], 256 * n + h[1]), b, S("Tf5", *h), A.not_equal)
+            if n < 5:
+                ts(S("vi", *h), S("t32", *h), 4095, A.bitwise_and)
+                flush()
+                cp(S("off", *h), S("vi", *h))
+                late.append(c)
+
+        def sum_ok(hf):
+            for ww in range(4):
+                o = 1536 + 128 * hf + 32 * ww
+                tt(S("NZ", o, o + 32), S("b1", 256 + 32 * hf, 288 + 32 * hf), S("shr", 4 * ww, 4 * ww + 32), A.is_le)
+
+        sums(0)
+        sums(2)
+        children(0)
+        for c in (0, 2, 1, 3):
+            equal(c)
+        sums(3)
+        children(2)
+        compare(0)
+        sums(1)
+        children(3)
+        spread("b1", 256, 64, "E", "Pg", 0, True, True)
+        spread("b1", 320, 16, "E", "Hl", 0, True, True)
+        total(0)
+        children(1)
+        diff(2)
+        diff(3)
+        sign(2)
+        total(2)
+        compare(1)
+        sign(3)
+        total(3)
+        total(1)
+        for n in range(5):
+            update(2, n)
+            gather_s(2)
+            update(0, n)
+            update(3, n)
+            gather_s(3)
+            flush()
+            diff(2)
+            compare(0)
+            total(0)
+            update(1, n)
+            if n == 0:
+                for k in range(3):
+                    ts(S("shr", 16 * k, 16 * k + 16), S("b1", 320, 336), -1.0, A.mult, S("kap2"), A.add)
+            if n in (1, 2):
+                sum_ok(n - 1)
+            flush()
+            diff(3)
+            sign(2)
+            total(2)
+            compare(1)
+            sign(3)
+            total(3)
+            if n < 4:
+                total(1)
+        act(S("Zf"), S("Zp", 2048, 4096), F.Identity, bias=32.0)
+
+        def tests(hf, ms):
+            for m in ms:
+                mm(S("b%d" % (4 + hf), 0, 128), S("ident"), S("NZ", 256 * m + 128 * hf, 256 * m + 128 * hf + 128), m == 6, m == 5)
+
+        def passed(hf):
+            ts(S("AL", 128 * hf, 128 * hf + 128), S("b%d" % (4 + hf), 0, 128), 7.0, A.is_equal)
+
+        def alive(hf):
+            bs, bx, a0 = "b%d" % (2 * hf), "b%d" % (2 * hf + 1), 128 * hf
+            al = [S("AL", a0 + 32 * ww, a0 + 32 * ww + 32) for ww in range(4)]
+            for ww in range(4):
+                mm(S(bx, 0, 32), S("Bones"), al[ww], ww == 0, ww == 3)
+            for ww in range(4):
+                mm(S(bx, 32, 64), S("Ds"), al[ww], ww == 0, ww == 3)
+            for ww in range(4):
+                mm(S(bs, 32 * ww, 32 * ww + 32), S("I16384"), al[ww], True, ww == 0)
+                for w2 in range(ww):
+                    mm(S(bs, 32 * ww, 32 * ww + 32), S("ident"), al[w2], False, w2 == ww - 1)
+
+        def number(hf):
+            bs, bx, a0 = "b%d" % (2 * hf), "b%d" % (2 * hf + 1), 128 * hf
+            sc, pb = S("sc", 32 * hf, 32 * hf + 32), S("pb", 32 * hf, 32 * hf + 32)
+            scan(sc, S(bx, 0, 32), 32)
+            tt(pb, sc, S(bx, 32, 64), A.add)
+            for ww in range(4):
+                tt(S("of", a0 + 32 * ww, a0 + 32 * ww + 32), S(bs, 32 * ww, 32 * ww + 32), pb, A.add)
+
+        def offsets(hf):
+            a0 = 128 * hf
+            tt(S("mx", a0, a0 + 128), S("of", a0, a0 + 128), S("KT"), A.max)
+            ts(S("so", a0, a0 + 128), S("mx", a0, a0 + 128), -14336.0, A.add)
+        tests(1, (6, 0, 1, 2, 3, 4))
+        update(0, 5)
+        update(2, 5)
+        update(3, 5)
+        tests(1, (5,))
+        total(1)
+        passed(1)
+        alive(1)
+        update(1, 5)
+        tests(0, (6, 0, 1, 2, 3, 4, 5))
+        number(1)
+        passed(0)
+        alive(0)
+        offsets(1)
+        act(IND(S("SAf"), S("so", 128, 256)), S("Zf"), F.Silu)
+        number(0)
+        offsets(0)
+        tt(S("nS"), S("sc", 31, 32), S("sc", 63, 64), A.add)
+        ts(S("dA"), S("sc", 31, 32), -1.0, A.mult, 2048.0, A.add)
+        ts(S("g2"), S("W3", 0, 256), S("nS"), A.is_gt, 8192.0, A.mult)
+        ts(S("g1"), S("W3", 0, 256), S("sc", 31, 32), A.is_gt, S("dA"), A.mult)
+        mm(S("b4", 0, 256), S("identF"), S("W3", 0, 256), True, False)
+        mm(S("b4", 0, 256), S("N16384"), S("Fl", 0, 256), False, False)
+        mm(S("b4", 0, 256), S("identF"), S("g2"), False, False)
+        mm(S("b4", 0, 256), S("identF"), S("g1"), False, True)
+        cp(IND(S(cur, 0, SA), S("so", 0, 128)), S("Zp", 0, 2048))
+        act(S(cur, SA, SA + 1216), S("SAf", 2048, 3264), F.Relu, bias=-32.0005)
+        tt(S("fo"), S("b4", 0, 256), S("VT"), A.min)
+        ts(S("fo16"), S("fo"), 16383.0, A.add)
+        ts(S(cur, SA + 1216, XO), S("SAf", 3264, 4096), MAGIC - 32.0, A.add, -MAGIC, A.add)
+
+        def place(b):
+            win = IND(S(cur, SV, XE), S("fo16", 32 * b, 32 * b + 32))
+            o = S(nxt, XO + 512 * b, XO + 512 * b + 512)
+            if t < 2:
+                if b % 2 == 0:
+                    cp(o, win)
+                else:
+                    act(o, win, F.Copy)
+            else:
+                if b % 2 == 0:
+                    ts(o, win, -1.0, A.mult, 255.0, A.add)
+                else:
+                    act(o, win, F.Identity, bias=255.0, scale=-1.0)
+                op("sync", lambda: g.sync.dma_start(T.y[:, 512 * b:512 * b + 512], AP(o)), [o], [], "ys%d" % b, 16)
+        for b in range(8):
+            place(b)
+    emit()

@@ -2,48 +2,54 @@ import numpy as np
 from concourse.bass import DstId, RemoteDMATransfer
 from concourse.mybir import dt, AluOpType as A, AxisListType, ActivationFunctionType as F
 
-SV, SA, XO, XE, BWC = 2048, 4096, 6144, 10240, 10272
+XE, XC = 4096, 4128
+SV, SS, FX, FE = 2048, 4096, 8192, 12288
 SB = {
-    "BW0": (BWC, "bfloat16"), "BW1": (BWC, "bfloat16"), "SAf": (4096, "float32"), "Zp": (4096, "bfloat16"),
+    "BW0": (XC, "bfloat16"), "BW1": (XC, "bfloat16"), "FW": (FE, "float32"), "Zp": (4096, "bfloat16"),
     "Zf": (2048, "float32"), "Pg": (1024, "bfloat16"), "Hs": (256, "bfloat16"), "Hl": (256, "bfloat16"),
     "c1n": (256, "bfloat16"), "c2n": (256, "bfloat16"), "c3n": (256, "bfloat16"),
     "c1p": (1024, "bfloat16"), "c2p": (1024, "bfloat16"), "c3p": (1024, "bfloat16"),
-    "cmp": (4096, "bfloat16"), "G": (2048, "bfloat16"), "acc": (8, "float32"),
-    "cown0": (1, "float32"), "cown1": (1, "float32"), "cown2": (1, "float32"),
-    "cl0": (4, "float32"), "cl1": (4, "float32"), "cl2": (4, "float32"),
-    "qi": (16, "int32"), "qf": (16, "float32"), "Qblk": (128, "bfloat16"), "kap16": (1, "float32"),
+    "cmp": (4096, "bfloat16"), "G": (2048, "bfloat16"), "dg": (128, "float32"),
+    "cown": (12, "float32"), "cl": (144, "float32"), "small": (16, "float32"), "lst": (160, "bfloat16"),
+    "qi": (16, "int32"), "qf": (16, "float32"), "Qblk": (128, "bfloat16"), "nQ4": (512, "bfloat16"), "kapT": (512, "float32"),
     "pi": (1, "int32"), "p16i": (1, "int32"), "pgi": (1, "int32"), "pif": (1, "float32"), "p16f": (1, "float32"),
     "pgf": (1, "float32"), "e15": (1, "float32"), "p37": (1, "float32"), "ci": (144, "int32"), "cg": (128, "int32"),
     "Bones": (128, "bfloat16"), "BonesF": (128, "float32"), "ident": (128, "bfloat16"), "identF": (128, "float32"),
-    "nident": (128, "bfloat16"), "I3856": (128, "bfloat16"), "I1928": (128, "bfloat16"), "I16384": (128, "bfloat16"),
-    "N16384": (128, "bfloat16"), "EM1": (144, "bfloat16"), "EM16": (144, "bfloat16"), "EM256": (144, "bfloat16"),
+    "nident": (128, "bfloat16"), "I3856": (128, "bfloat16"), "I16384": (128, "bfloat16"), "I8192": (128, "bfloat16"),
+    "N16384": (128, "bfloat16"), "EM1": (144, "bfloat16"), "I16": (128, "bfloat16"),
     "EM241": (144, "bfloat16"), "EM120": (144, "bfloat16"), "E": (144, "bfloat16"), "M16f": (16, "float32"),
-    "mask16": (16, "float32"), "base": (16, "float32"), "obig": (16, "float32"), "rown": (16, "float32"),
-    "rpeer": (16, "float32"), "Dm": (128, "bfloat16"), "Ds": (128, "bfloat16"), "dtmp": (128, "bfloat16"),
-    "B255": (128, "bfloat16"), "col255": (1, "bfloat16"), "Ji": (602, "int32"), "Jm": (602, "int32"), "JF": (602, "float32"),
+    "mask16": (16, "float32"), "base": (16, "float32"), "obig": (16, "float32"), "rown": (48, "float32"),
+    "Dm": (128, "bfloat16"), "Ds": (128, "bfloat16"), "dtmp": (128, "bfloat16"),
+    "B4080": (128, "bfloat16"), "c4080": (128, "bfloat16"), "Ji": (602, "int32"), "Jm": (602, "int32"), "JF": (602, "float32"),
     "IF": (1024, "float32"), "IU": (1024, "uint16"), "JTi": (384, "int32"), "JTk": (384, "int32"), "JTm": (384, "int32"),
     "JT": (384, "float32"), "VTi": (256, "int32"), "VT": (256, "float32"), "KT": (128, "float32"),
-    "onesF": (256, "float32"), "onesB": (64, "bfloat16"), "W2": (48, "float32"), "W3": (528, "float32"),
-    "t3": (1, "float32"), "mn": (1, "float32"), "oh": (16, "float32"), "cq": (16, "float32"), "csel": (1, "float32"),
+    "onesF": (256, "float32"), "W2": (48, "float32"), "W3": (528, "float32"),
+    "mn": (1, "float32"), "oh": (16, "float32"), "cq": (16, "float32"), "csel": (1, "float32"),
     "csb": (1, "bfloat16"), "kaps": (1, "float32"), "kap2": (1, "float32"), "Fl": (512, "bfloat16"), "T2b": (32, "bfloat16"),
     "I3": (512, "float32"), "I2": (32, "float32"), "bt": (32, "float32"), "bnd": (8, "float32"),
     "oAn": (16, "uint16"), "oQn": (16, "uint16"), "oPn": (16, "uint16"), "oAp": (64, "uint16"), "oQp": (64, "uint16"),
-    "oPp": (64, "uint16"), "A17": (64, "float32"),
+    "oPp": (64, "uint16"), "A17": (64, "float32"), "AF": (64, "float32"),
     "t32": (256, "int32"), "vi": (256, "int32"), "off": (256, "uint16"), "Tf5": (256, "float32"), "eq": (256, "bfloat16"),
     "NZ": (1792, "bfloat16"), "shr": (48, "float32"), "AL": (256, "bfloat16"), "sc": (64, "float32"), "pb": (64, "float32"),
-    "of": (256, "float32"), "mx": (256, "float32"), "so": (256, "uint16"), "nS": (1, "float32"), "dA": (1, "float32"),
-    "g1": (256, "float32"), "g2": (256, "float32"), "fo": (256, "float32"), "fo16": (256, "uint16"),
+    "of": (256, "float32"), "mx": (256, "float32"), "so": (256, "uint16"),
+    "g1": (256, "float32"), "g2": (256, "bfloat16"), "fo": (256, "float32"), "fo16": (256, "uint16"),
 }
+PART = {"lAn": ("lst", 0, 16), "lQn": ("lst", 16, 16), "lAp": ("lst", 32, 64), "lQp": ("lst", 96, 64),
+        "m05": ("small", 0, 1), "nT": ("small", 4, 1), "nS": ("small", 8, 1), "dA": ("small", 12, 1)}
+for _t in range(3):
+    PART["cown%d" % _t] = ("cown", 4 * _t, 1)
+    PART["rown%d" % _t] = ("rown", 16 * _t, 16)
+    PART["cl%d" % _t] = ("cl", 48 * _t, 48)
 SCRATCH = {n: ("sbuf", [128, -(-c // 16) * 16], d) for n, (c, d) in SB.items()}
 for _b in range(8):
     SCRATCH["b%d" % _b] = ("psum", [128, 512], "float32")
 NX = 8
 QSEM = {"tensor": "sT", "vector": "sV", "scalar": "sS", "g": "sG"}
 SEMAPHORES = (["sT", "sV", "sS", "sG", "qld"] + ["xl%d" % i for i in range(NX)] + ["ys%d" % i for i in range(8)]
-              + ["%s%d" % (s, t) for s in ("cs", "gs", "lc", "lg") for t in range(3)])
+              + ["%s%d" % (s, t) for s in ("cs", "gs", "lc", "lg", "fx", "fz") for t in range(3)])
 XS = (1, 2, 3)
 BIG = 1048576.0
-MAGIC = 8388608.0
+LOOP = "a2 b2 o2 a0 g2 e2 b0 a3 x2 b3 y2 o0 o3 c0 a1 g3 e0 u2 v2 b1 e3 s y3 v3 x3 o1 t2 e1 u3 t0 c1 t3 t1"
 CE = 4
 
 
@@ -51,9 +57,9 @@ def make_queue(g, T):
     ops, hist = [], {}
     eng = {"tensor": g.tensor, "vector": g.vector, "scalar": g.scalar, "sync": g.sync, "g": g}
 
-    def op(q, fn, reads, writes, sem=None, val=0):
+    def op(q, fn, reads, writes, sem=None, val=0, remote=False):
         me = len(ops)
-        rec = {"q": q, "fn": fn, "deps": set(), "sem": sem, "val": val, "need": False, "m": []}
+        rec = {"q": q, "fn": fn, "deps": set(), "sem": sem, "val": val, "need": False, "m": [], "remote": remote}
         acc = []
         for w in writes:
             if w[0] == "IND":
@@ -124,7 +130,7 @@ def make_queue(g, T):
                 c = dict(k)
                 c[r["sem"]] = r["val"]
                 c["own"] = r["sem"]
-                if q != "g":
+                if not r["remote"]:
                     ins.then_inc(T.sem[r["sem"]], r["val"])
             else:
                 s = QSEM[q]
@@ -153,8 +159,8 @@ def rank_program(g, core, T, topo):
     op, emit = make_queue(g, T)
 
     def S(n, a=0, b=None, st=1):
-        if b is None:
-            b = SB[n][0] if n in SB else 512
+        n, o, w = PART.get(n, (n, 0, SB[n][0] if n in SB else 512))
+        a, b = a + o, (w if b is None else b) + o
         return (n, a, b, T[n][:, a:b] if st == 1 else T[n][:, a:b:st])
 
     def IND(w, o):
@@ -191,14 +197,13 @@ def rank_program(g, core, T, topo):
     def fill(out, c):
         op("vector", lambda: g.vector.memset(AP(out), c), [], [out])
 
-    def act(out, a, f, bias=0.0, scale=1.0, accum=None):
-        if accum is None:
-            if f == F.Silu:
-                op("scalar", lambda: g.scalar.activation(AP(out), AP(a), f), [a], [out])
-            else:
-                op("scalar", lambda: g.scalar.activation(AP(out), AP(a), f, bias=bias, scale=scale), [a], [out])
+    def act(out, a, f, bias=0.0, scale=1.0):
+        if f == F.Silu:
+            op("scalar", lambda: g.scalar.activation(AP(out), AP(a), f), [a], [out])
         else:
-            op("scalar", lambda: g.scalar.activation(AP(out), AP(a), f, accum_out=AP(accum)), [a], [out, accum])
+            cols = [x for x in (bias, scale) if not num(x)]
+            ub, us = bias if num(bias) else AP(bias), scale if num(scale) else AP(scale)
+            op("scalar", lambda: g.scalar.activation(AP(out), AP(a), f, bias=ub, scale=us), [a] + cols, [out])
 
     def mm(out, l, r, start, stop):
         op("tensor", lambda: g.tensor.matmul(AP(out), AP(l), AP(r), start, stop), [l, r], [out])
@@ -213,11 +218,14 @@ def rank_program(g, core, T, topo):
         else:
             op("g", lambda: g.iota(AP(out), pattern, base, cm), [], [out])
 
+    def cast_in(out, in_ap, reads, sem):
+        op("g", lambda: g.dma_start(AP(out), in_ap), reads, [out], sem, 16)
+
     op("sync", lambda: g.sync.dma_start(T.qi[:, 0:16], T.q[:]), [], [S("qi")], "qld", 16)
     w = 4096 // NX
 
     def load(i, q):
-        o = S("BW1", XO + w * i, XO + w * i + w)
+        o = S("BW1", w * i, w * i + w)
         op(q, lambda: (g.sync if q == "sync" else g.scalar).dma_start(AP(o), T.x[:, w * i:w * i + w]), [], [o], "xl%d" % i, 16)
     for i in range(NX):
         load(i, "sync" if i % 2 else "scalar")
@@ -226,20 +234,21 @@ def rank_program(g, core, T, topo):
     iota(S("Ji"), [[37, 602]])
     iota(S("IF"), [[1, 1024]], 0, 0, True)
     iota(S("JTi"), [[1, 3], [64, 4], [592, 32]])
-    iota(S("VTi"), [[16, 256]], 4096)
-    ts(S("p16i"), S("pi"), 15, A.bitwise_and)
+    iota(S("VTi"), [[16, 256]], FX - SV)
+    iota(S("KT"), [[16, 128]], 16384 - SV, 0, True)
     ts(S("pgi"), S("pi"), 4, A.arith_shift_right)
-    cp(S("pif"), S("pi"))
     ts(S("cg"), S("ci", 0, 128), 4, A.arith_shift_right)
+    ts(S("p16i"), S("pi"), 15, A.bitwise_and)
     cp(S("pgf"), S("pgi"))
+    cp(S("pif"), S("pi"))
     cp(S("p16f"), S("p16i"))
     ts(S("BonesF"), S("cg"), S("pgf"), A.is_equal)
-    ts(S("M16f"), S("ci", 0, 16), S("p16f"), A.is_equal, 16.0, A.mult)
     ts(S("identF"), S("ci", 0, 128), S("pif"), A.is_equal)
-    cp(S("base"), S("ci", 0, 16))
-    tt(S("e15"), S("pif"), S("p16f"), A.subtract)
     for k in range(8):
         ts(S("Qblk", 16 * k, 16 * k + 16), S("qi"), S("BonesF", 16 * k, 16 * k + 1), A.mult)
+    ts(S("M16f"), S("ci", 0, 16), S("p16f"), A.is_equal, 16.0, A.mult)
+    cp(S("base"), S("ci", 0, 16))
+    tt(S("e15"), S("pif"), S("p16f"), A.subtract)
 
     def consts_a():
         ts(S("e15"), S("e15"), 15.0, A.add)
@@ -247,19 +256,18 @@ def rank_program(g, core, T, topo):
         ts(S("dtmp"), S("ci", 0, 128), S("pif"), A.is_lt, -1.0, A.mult)
         ts(S("EM1"), S("ci"), S("e15"), A.is_equal)
         act(S("Bones"), S("BonesF"), F.Copy)
-        act(S("B255"), S("BonesF"), F.Copy, scale=255.0)
+        act(S("B4080"), S("BonesF"), F.Copy, scale=4080.0)
         act(S("ident"), S("identF"), F.Copy)
         tt(S("Dm"), S("dtmp"), S("BonesF"), A.mult)
-        for n, s in (("EM16", 16.0), ("EM256", 256.0)):
-            act(S(n), S("EM1"), F.Copy, scale=s)
+        act(S("I16"), S("identF"), F.Copy, scale=16.0)
         for b in range(8):
-            o, i = S("BW0", XO + 512 * b, XO + 512 * b + 512), S("BW1", XO + 512 * b, XO + 512 * b + 512)
+            o, i = S("BW0", 512 * b, 512 * b + 512), S("BW1", 512 * b, 512 * b + 512)
             if b in (2, 5, 7):
-                act(o, i, F.Identity, bias=255.0, scale=-1.0)
+                act(o, i, F.Identity, bias=4080.0, scale=-16.0)
             else:
-                ts(o, i, -1.0, A.mult, 255.0, A.add)
-        fill(S("BW0", XE, BWC), 0.0)
-        fill(S("BW1", XE, BWC), 0.0)
+                ts(o, i, -16.0, A.mult, 4080.0, A.add)
+        fill(S("BW0", XE, XC), 0.0)
+        fill(S("BW1", XE, XC), 0.0)
         ts(S("mask16"), S("M16f"), 0.0625, A.mult)
         fill(S("onesF"), 1.0)
         for a, b in ((16, 24), (40, 48)):
@@ -270,29 +278,33 @@ def rank_program(g, core, T, topo):
     def consts_b():
         for n, s in (("EM241", 241.0), ("EM120", 120.5)):
             act(S(n), S("EM1"), F.Copy, scale=s)
-        for n, s in (("nident", -1.0), ("I3856", 3856.0), ("I1928", 1928.0), ("I16384", 16384.0), ("N16384", -16384.0)):
+        for n, s in (("nident", -1.0), ("I3856", 3856.0), ("I16384", 16384.0), ("I8192", 8192.0), ("N16384", -16384.0)):
             act(S(n), S("identF"), F.Copy, scale=s)
-        act(S("SAf", 2048, 4096), S("BW1", XO, XO + 2048), F.Copy)
-        act(S("BW0", SV, SA), S("BW1", XO, XO + 2048), F.Copy)
+        for k in range(3):
+            act(S("FW", SV + 2048 * k, SV + 2048 * k + 2048), S("BW1", 0, 2048), F.Copy)
         ts(S("Jm"), S("Ji"), 255, A.bitwise_and)
+        fill(S("m05"), -0.5)
         ts(S("p37"), S("p16f"), 37.0, A.mult)
         cp(S("JF"), S("Jm"))
 
     def consts_c():
         ts(S("JTk"), S("JTi"), S("p37"), A.add)
-        fill(S("col255"), 255.0)
-        tt(S("Ds"), S("Dm"), S("identF"), A.subtract)
         ts(S("JTm"), S("JTk"), 255, A.bitwise_and)
-        fill(S("onesB"), 1.0)
-        ts(S("VT"), S("VTi"), S("p16f"), A.add, -16383.0, A.add)
-        ts(S("JT"), S("JTm"), 5.0, A.mult)
-        ts(S("KT"), S("VT", 0, 128), 26623.0, A.add)
-        mm(S("b2", 0, 1), S("Qblk"), S("col255"), True, True)
-        cp(S("kap16"), S("b2", 0, 1))
+
+    def consts_f():
+        tt(S("Ds"), S("Dm"), S("identF"), A.subtract)
+        ts(S("VT"), S("VTi"), S("p16f"), A.add, -24575.0, A.add)
+        ts(S("KT"), S("KT"), S("p16f"), A.add)
 
     def consts_d():
         cp(S("IU"), S("IF"))
-        act(S("BW1", SV, SA), S("BW0", XO, XO + 2048), F.Copy)
+
+    def consts_e():
+        for k in range(4):
+            act(S("nQ4", 128 * k, 128 * k + 128), S("Qblk"), F.Copy, scale=-1.0)
+        fill(S("c4080"), 4080.0)
+        mm(S("b5"), S("c4080"), S("nQ4"), True, True)
+        act(S("kapT"), S("b5"), F.Copy, scale=-1.0)
 
     peers = [r for r in range(len(T.cores)) if r != rank]
     peers.sort(key=lambda r: len(topo.engines(core, T.cores[r])))
@@ -309,9 +321,9 @@ def rank_program(g, core, T, topo):
                 rid, pid, _s = topo.addr(T.cores[r])
                 c = [k for k in range(len(T.cores)) if k != r].index(rank)
                 tr.append(RemoteDMATransfer(dst_ids=[DstId(rid=rid, pnc=pid)], dma_engine_mask=m, remote_sem=T.sem["cs%d" % t],
-                                            src=T["cown%d" % t][:, 0:1], dst=T["cl%d" % t][:, c:c + 1]))
+                                            src=AP(S("rown%d" % t)), dst=AP(S("cl%d" % t, 16 * c, 16 * c + 16))))
             return g.remote_dma_fused(tr, local_sem=T.sem["lc%d" % t])
-        op("g", f, [S("cown%d" % t)], [], "lc%d" % t, CE * len(peers))
+        op("g", f, [S("rown%d" % t)], [], "lc%d" % t, CE * len(peers), True)
         op(None, None, [], [S("cl%d" % t)], "cs%d" % t, CE * len(peers))
 
     def send_guests(t):
@@ -321,42 +333,66 @@ def rank_program(g, core, T, topo):
         def f():
             rid, pid, _s = topo.addr(dst)
             return g.remote_dma(T.Hl[:, 0:256], T.Hs[:, 0:256], T.sem["gs%d" % t], T.sem["lg%d" % t], pid, rid, sum(1 << e for e in es))
-        op("g", f, [S("Hs")], [], "lg%d" % t, len(es))
+        op("g", f, [S("Hs")], [], "lg%d" % t, len(es), True)
 
     def guests_come(t):
         src = T.cores[rank ^ XS[t]]
         op(None, None, [], [S("Hl")], "gs%d" % t, len(topo.engines(src, core)[:8]))
 
+    def values(t, b):
+        xs, bank = "BW1" if t < 2 else "BW0", "b%d" % (b % 7)
+        shift = t > 0 and b % 2 == 1
+        if shift:
+            mm(S(bank), S("c4080"), S("nQ4"), True, False)
+        for k in range(4):
+            mm(S(bank, 128 * k, 128 * k + 128), S(xs, 512 * b + 128 * k, 512 * b + 128 * k + 128), S("Qblk"), not shift,
+               not shift or k == 3)
+
+    def nonzero(t, b):
+        bank, o = S("b%d" % (b % 7)), S("cmp", 512 * b, 512 * b + 512)
+        if b % 2 == 1:
+            act(o, bank, F.Sign)
+        elif t == 0:
+            ts(o, bank, 0.0, A.not_equal)
+        else:
+            tt(o, bank, S("kapT"), A.not_equal)
+
+    def diagonal(b):
+        for k in range(4):
+            c = S("cmp", 512 * b + 128 * k, 512 * b + 128 * k + 128)
+            mm(S("b7", 0, 128), c, c, b == 0 and k == 0, b == 7 and k == 3)
+
+    for b in range(4):
+        values(0, b)
+    for b in range(8):
+        nonzero(0, b)
+        diagonal(b)
+        if b < 4:
+            values(0, b + 4)
     for t in range(3):
         cur, nxt = ("BW0", "BW1") if t % 2 == 0 else ("BW1", "BW0")
-        xs = "BW1" if t == 0 else cur
-        X = S(cur, XO, BWC)
-        for b in range(8):
-            sl = (512 * b, 512 * b + 512)
-            mm(S("b%d" % b), S("Qblk"), S(xs, XO + sl[0], XO + sl[1]), True, True)
-            ts(S("cmp", *sl), S("b%d" % b), 0.0 if t == 0 else S("kap16"), A.not_equal)
-            act(S("G", 512 * (b % 4), 512 * (b % 4) + 512), S("cmp", *sl), F.Copy, accum=S("acc", b, b + 1))
-        cown, cl = S("cown%d" % t), S("cl%d" % t, 0, 3)
-        red(cown, S("acc"), A.add)
+        X = S(cur, 0, XC)
+        cown, rown = S("cown%d" % t), S("rown%d" % t)
+        tt(S("dg"), S("b7", 0, 128), S("identF"), A.mult)
+        red(cown, S("dg"), A.add)
+        ts(rown, S("M16f"), cown, A.mult)
         send_counts(t)
-        ts(S("rown"), S("M16f"), cown, A.mult)
         mm(S("b0", 0, 16), S("identF"), S("base"), True, False)
-        mm(S("b0", 0, 16), S("BonesF"), S("rown"), False, False)
+        mm(S("b0", 0, 16), S("BonesF"), rown, False, False)
         if t == 0:
             consts_a()
         if t == 1:
             consts_d()
-        red(S("t3"), cl, A.add)
-        ts(S("rpeer"), S("M16f"), S("t3"), A.mult)
-        mm(S("b0", 0, 16), S("BonesF"), S("rpeer"), False, True)
+        for k in range(3):
+            mm(S("b0", 0, 16), S("BonesF"), S("cl%d" % t, 16 * k, 16 * k + 16), False, k == 2)
         red(S("mn"), S("b0", 0, 16), A.min)
         ts(S("oh"), S("b0", 0, 16), S("mn"), A.is_equal)
         tt(S("cq"), S("oh"), S("qf"), A.mult)
         red(S("csel"), S("cq"), A.add)
         ts(S("E"), S("EM1"), S("csel"), A.mult)
         cp(S("csb"), S("csel"))
-        mm(S("b1", 0, 1), S("B255"), S("csb"), True, True)
-        spread("b2", 0, 256, "E", cur, XO, True, True)
+        mm(S("b1", 0, 1), S("B4080"), S("csb"), True, True)
+        spread("b2", 0, 256, "E", cur, 0, True, True)
         cp(S("kaps"), S("b1", 0, 1))
         ts(S("obig"), S("oh"), BIG, A.mult)
         ts(S("kap2"), S("kaps"), 2.0, A.mult)
@@ -369,6 +405,8 @@ def rank_program(g, core, T, topo):
             mm(S("b3", 0, 32), S("EM1", 15 - p, 143 - p), S("Fl", p, 512, 16), p == 0, p == 15)
         mm(S("b4"), S("Bones"), S("Fl"), True, True)
         mm(S("b5"), S("Dm"), S("Fl"), True, True)
+        if t == 0:
+            consts_c()
         cp(S("T2b"), S("b3", 0, 32))
         mm(S("b6", 0, 32), S("Bones"), S("T2b"), True, True)
         mm(S("b6", 32, 64), S("Dm"), S("T2b"), True, True)
@@ -382,61 +420,86 @@ def rank_program(g, core, T, topo):
         J = S("JF", 173 * t, 173 * t + 256)
         ts(S("c1n"), J, S("bnd", 0, 1), A.is_ge)
         spread("b7", 0, 16, "EM1", "c1n", 0, True, True)
-        spread("b0", 0, 16, "EM16", "c1n", 0, True, False)
+        ts(S("c1p"), S("IF" if t == 0 else "IU"), S("bnd", 4, 5), A.is_ge)
+        spread("b1", 0, 64, "EM1", "c1p", 0, True, True)
         tt(S("W2", 0, 16), S("I2", 0, 16), S("b6", 32, 48), A.add)
         tt(S("W2", 24, 40), S("I2", 16, 32), S("b6", 48, 64), A.add)
-        tt(S("W3", 0, 256), S("I3", 0, 256), S("b5", 0, 256), A.add)
         cp(S("oAn"), S("b7", 0, 16))
+        act(S("lAn"), S("b7", 0, 16), F.Copy)
         tt(S("c2n"), IND(S("W2", 0, 24), S("oAn")), J, A.is_le)
+        mm(S("b0", 0, 16), S("I16"), S("lAn"), True, False)
         spread("b0", 0, 16, "EM1", "c2n", 0, False, True)
-        spread("b3", 0, 16, "EM256", "c1n", 0, True, False)
-        spread("b3", 0, 16, "EM16", "c2n", 0, False, False)
-        ts(S("c1p"), S("IF" if t == 0 else "IU"), S("bnd", 4, 5), A.is_ge)
+        tt(S("W3", 0, 256), S("I3", 0, 256), S("b5", 0, 256), A.add)
+        cp(S("oAp"), S("b1", 0, 64))
+        act(S("lAp"), S("b1", 0, 64), F.Copy)
+        qb, pbk = ("b6", "b2"), ("b7", "b1")
+
+        def find2(h):
+            o, k = (512 * h, 512 * h + 512), (32 * h, 32 * h + 32)
+            tt(S("c2p", *o), IND(S("W2", 24, 48), S("oAp", *k)), S("IF", *o), A.is_le)
+            mm(S(qb[h], 0, 32), S("I16"), S("lAp", *k), True, False)
+            spread(qb[h], 0, 32, "EM1", "c2p", 512 * h, False, True)
+
+        def find3(h):
+            o, k = (512 * h, 512 * h + 512), (32 * h, 32 * h + 32)
+            cp(S("oQp", *k), S(qb[h], 0, 32))
+            act(S("lQp", *k), S(qb[h], 0, 32), F.Copy)
+            tt(S("c3p", *o), IND(S("W3", 264, 528), S("oQp", *k)), S("IF", *o), A.is_le)
+            mm(S(pbk[h], 0, 32), S("I16"), S("lQp", *k), True, False)
+            spread(pbk[h], 0, 32, "EM1", "c3p", 512 * h, False, True)
+
+        def start(h):
+            k = (32 * h, 32 * h + 32)
+            cp(S("oPp", *k), S(pbk[h], 0, 32))
+            ts(S("A17", *k), S(pbk[h], 0, 32), 17.0, A.mult)
+            cp(S("AF", *k), S(pbk[h], 0, 32))
+            act(S("Pg", 512 * h, 512 * h + 512), IND(X, S("oPp", *k)), F.Copy)
+            for ww in range(4):
+                o = 128 * h + 32 * ww
+                tt(S("t32", o, o + 32), S("A17", *k), S("JT", 128 * t + 32 * ww, 128 * t + 32 * ww + 32), A.add)
+            o = (128 * h, 128 * h + 128)
+            ts(S("vi", *o), S("t32", *o), 4095, A.bitwise_and)
+            cp(S("off", *o), S("vi", *o))
+
+        def own_places(h):
+            for c in (2 * h, 2 * h + 1):
+                for k in range(2):
+                    mm(S("b%d" % c, 384 + 32 * k, 416 + 32 * k), S("identF"), S("AF", 32 * h, 32 * h + 32), True, True)
         cp(S("oQn"), S("b0", 0, 16))
+        act(S("lQn"), S("b0", 0, 16), F.Copy)
         tt(S("c3n"), IND(S("W3", 0, 264), S("oQn")), J, A.is_le)
+        mm(S("b3", 0, 16), S("I16"), S("lQn"), True, False)
         spread("b3", 0, 16, "EM1", "c3n", 0, False, True)
-        spread("b1", 0, 64, "EM1", "c1p", 0, True, True)
-        spread("b6", 0, 64, "EM16", "c1p", 0, True, False)
         scan(S("I3", 256, 512), S("b4", 256, 512), 256)
+        find2(0)
+        tt(S("W3", 264, 520), S("I3", 256, 512), S("b5", 256, 512), A.add)
         cp(S("oPn"), S("b3", 0, 16))
         act(S("Hs"), IND(X, S("oPn")), F.Copy)
         send_guests(t)
-        cp(S("oAp"), S("b1", 0, 64))
-        tt(S("c2p"), IND(S("W2", 24, 48), S("oAp")), S("IF"), A.is_le)
-        spread("b6", 0, 64, "EM1", "c2p", 0, False, True)
-        spread("b7", 0, 64, "EM256", "c1p", 0, True, False)
-        tt(S("W3", 264, 520), S("I3", 256, 512), S("b5", 256, 512), A.add)
-        spread("b7", 0, 64, "EM16", "c2p", 0, False, False)
+        find2(1)
+        find3(0)
+        find3(1)
         if t == 0:
-            consts_c()
-        cp(S("oQp"), S("b6", 0, 64))
-        tt(S("c3p"), IND(S("W3", 264, 528), S("oQp")), S("IF"), A.is_le)
-        spread("b7", 0, 64, "EM1", "c3p", 0, False, True)
-        cp(S("oPp"), S("b7", 0, 64))
-        ts(S("A17"), S("b7", 0, 64), 17.0, A.mult)
-        for hf in range(2):
-            act(S("Pg", 512 * hf, 512 * hf + 512), IND(X, S("oPp", 32 * hf, 32 * hf + 32)), F.Copy)
-        for hf in (0, 1):
-            for ww in range(4):
-                o = 128 * hf + 32 * ww
-                tt(S("t32", o, o + 32), S("A17", 32 * hf, 32 * hf + 32), S("JT", 128 * t + 32 * ww, 128 * t + 32 * ww + 32), A.add)
-            h = (128 * hf, 128 * hf + 128)
-            ts(S("vi", *h), S("t32", *h), 4095, A.bitwise_and)
-            cp(S("off", *h), S("vi", *h))
-        for c in range(4):
-            for k in range(2):
-                act(S("b%d" % c, 128 + 32 * k, 160 + 32 * k), S("b7", 32 * (c // 2), 32 * (c // 2) + 32), F.Copy)
+            ts(S("JT"), S("JTm"), 5.0, A.mult)
+        start(0)
+        own_places(0)
+        start(1)
+        own_places(1)
+        if t == 0:
+            consts_f()
+            consts_e()
 
         def gather_s(c):
             act(S("G", 1024 * (c - 2), 1024 * (c - 2) + 1024), IND(X, S("off", 64 * c, 64 * c + 64)), F.Copy)
 
         def equal(c):
             h = (64 * c, 64 * c + 64)
-            ts(S("Tf5", *h), S("vi", *h), 5.0, A.mult, 1.0, A.add)
-            tt(S("eq", *h), S("vi", *h), S("b%d" % c, 128, 192), A.is_equal)
+            ts(S("Tf5", *h), S("vi", *h), 5.0, A.mult, 1.0 if c < 2 else 1929.0, A.add)
+            tt(S("eq", *h), S("vi", *h), S("b%d" % c, 384, 448), A.is_equal)
         gather_s(2)
         gather_s(3)
         guests_come(t)
+        cast_in(S("FW", FX, FE), T[cur][:, 0:4096], [S(cur, 0, XE), S("Hl")], "fx%d" % t)
         ub = {0: 4, 1: 6, 2: 6, 3: 4}
 
         def sums(c):
@@ -454,56 +517,49 @@ def rank_program(g, core, T, topo):
                 b = S("b%d" % (ub[c] + k))
                 o = S("Zp", 1024 * c + 512 * k, 1024 * c + 512 * k + 512)
                 if c == 3:
-                    act(o, b, F.Relu, bias=-255.0)
+                    act(o, b, F.Relu, bias=-4080.0)
                 else:
-                    ts(o, b, -255.0, A.add, 0.0, A.max)
+                    ts(o, b, -4080.0, A.add, 0.0, A.max)
 
-        def diff(c):
-            for k in range(2):
+        def diff(c, ks=(0, 1)):
+            for k in ks:
                 b = "b%d" % (2 * c + k)
                 o = 1024 * (c - 2) + 512 * k
                 mm(S(b), S("ident"), S("Zp", 1024 * c + 512 * k, 1024 * c + 512 * k + 512), True, False)
                 mm(S(b), S("nident"), S("G", o, o + 512), False, True)
 
-        def sign(c):
-            for k in range(2):
+        def sign(c, ks=(0, 1)):
+            for k in ks:
                 o = 1024 * c + 512 * k
                 act(S("cmp", o, o + 512), S("b%d" % (2 * c + k)), F.Sign, bias=-0.5)
 
         def compare(c):
             tt(S("cmp", 1024 * c, 1024 * c + 1024), IND(X, S("off", 64 * c, 64 * c + 64)), S("Zp", 1024 * c, 1024 * c + 1024), A.is_lt)
 
-        def total(c):
+        def total(c, n):
             b = "b%d" % c
-            h = (64 * c, 64 * c + 64)
-            mm(S(b, 0, 64), S("identF"), S("Tf5", *h), True, False)
-            mm(S(b, 0, 64), S("I3856"), S("eq", *h), False, False)
-            if c >= 2:
-                mm(S(b, 0, 64), S("I1928"), S("onesB"), False, False)
-            spread(b, 0, 64, "EM241" if c < 2 else "EM120", "cmp", 1024 * c, False, True)
-
-        late = []
-
-        def flush():
-            while late:
-                equal(late.pop())
+            mm(S(b, 64 * n, 64 * n + 64), S("I3856"), S("eq", 64 * c, 64 * c + 64), True, False)
+            spread(b, 64 * n, 64, "EM241" if c < 2 else "EM120", "cmp", 1024 * c, False, True)
 
         def update(c, n):
-            b = S("b%d" % c, 0, 64)
             h = (64 * c, 64 * c + 64)
-            if n < 5:
-                cp(S("t32", *h), b)
-            tt(S("NZ", 256 * n + h[0], 256 * n + h[1]), b, S("Tf5", *h), A.not_equal)
-            if n < 5:
-                ts(S("vi", *h), S("t32", *h), 4095, A.bitwise_and)
-                flush()
-                cp(S("off", *h), S("vi", *h))
-                late.append(c)
+            tt(S("t32", *h), S("b%d" % c, 64 * n, 64 * n + 64), S("Tf5", *h), A.add)
+
+        def wrap(c):
+            h = (64 * c, 64 * c + 64)
+            ts(S("vi", *h), S("t32", *h), 4095, A.bitwise_and)
+
+        def offs(c):
+            h = (64 * c, 64 * c + 64)
+            cp(S("off", *h), S("vi", *h))
+
+        def passed_probes(c, n0, n1):
+            ts(S("NZ", 384 * c + 64 * n0, 384 * c + 64 * n1), S("b%d" % c, 64 * n0, 64 * n1), 0.0 if c < 2 else -1928.0, A.not_equal)
 
         def sum_ok(hf):
             for ww in range(4):
                 o = 1536 + 128 * hf + 32 * ww
-                tt(S("NZ", o, o + 32), S("b1", 256 + 32 * hf, 288 + 32 * hf), S("shr", 4 * ww, 4 * ww + 32), A.is_le)
+                tt(S("NZ", o, o + 32), S("b1", 448 + 32 * hf, 480 + 32 * hf), S("shr", 4 * ww, 4 * ww + 32), A.is_le)
 
         sums(0)
         sums(2)
@@ -512,51 +568,48 @@ def rank_program(g, core, T, topo):
             equal(c)
         sums(3)
         children(2)
-        compare(0)
-        sums(1)
         children(3)
-        spread("b1", 256, 64, "E", "Pg", 0, True, True)
-        spread("b1", 320, 16, "E", "Hl", 0, True, True)
-        total(0)
-        children(1)
+        sums(1)
         diff(2)
+        compare(0)
+        children(1)
         diff(3)
         sign(2)
-        total(2)
+        total(2, 0)
+        total(0, 0)
         compare(1)
         sign(3)
-        total(3)
-        total(1)
+        total(3, 0)
+        total(1, 0)
+        cast_in(S("Zf"), T.Zp[:, 2048:4096], [S("Zp", 2048, 4096)], "fz%d" % t)
+        do = {"a": update, "b": lambda c, n: wrap(c), "o": lambda c, n: offs(c), "e": lambda c, n: equal(c),
+              "g": lambda c, n: gather_s(c), "c": lambda c, n: compare(c), "t": lambda c, n: total(c, n + 1),
+              "x": lambda c, n: diff(c, (0,)), "y": lambda c, n: diff(c, (1,)),
+              "u": lambda c, n: sign(c, (0,)), "v": lambda c, n: sign(c, (1,))}
         for n in range(5):
-            update(2, n)
-            gather_s(2)
-            update(0, n)
-            update(3, n)
-            gather_s(3)
-            flush()
-            diff(2)
-            compare(0)
-            total(0)
-            update(1, n)
-            if n == 0:
-                for k in range(3):
-                    ts(S("shr", 16 * k, 16 * k + 16), S("b1", 320, 336), -1.0, A.mult, S("kap2"), A.add)
-            if n in (1, 2):
-                sum_ok(n - 1)
-            flush()
-            diff(3)
-            sign(2)
-            total(2)
-            compare(1)
-            sign(3)
-            total(3)
-            if n < 4:
-                total(1)
-        act(S("Zf"), S("Zp", 2048, 4096), F.Identity, bias=32.0)
+            for k in LOOP.split():
+                if k == "s":
+                    if n == 0:
+                        spread("b1", 448, 64, "E", "Pg", 0, True, True)
+                        spread("b0", 448, 16, "E", "Hl", 0, True, True)
+                        for m in range(3):
+                            ts(S("shr", 16 * m, 16 * m + 16), S("b0", 448, 464), -1.0, A.mult, S("kap2"), A.add)
+                    elif n < 3:
+                        sum_ok(n - 1)
+                    else:
+                        for c in ((0, 2), (1, 3))[n - 3]:
+                            passed_probes(c, 0, n + 1)
+                elif (k, n) != ("t1", 4):
+                    do[k[0]](int(k[1]), n)
 
-        def tests(hf, ms):
-            for m in ms:
-                mm(S("b%d" % (4 + hf), 0, 128), S("ident"), S("NZ", 256 * m + 128 * hf, 256 * m + 128 * hf + 128), m == 6, m == 5)
+        def tests(hf, early):
+            b = "b%d" % (4 + hf)
+            if early:
+                mm(S(b, 0, 128), S("ident"), S("NZ", 1536 + 128 * hf, 1664 + 128 * hf), True, False)
+            for n in (range(4) if early else (4, 5)):
+                for k in range(2):
+                    o = 384 * (2 * hf + k) + 64 * n
+                    mm(S(b, 64 * k, 64 * k + 64), S("ident"), S("NZ", o, o + 64), False, n == 5 and k == 1)
 
         def passed(hf):
             ts(S("AL", 128 * hf, 128 * hf + 128), S("b%d" % (4 + hf), 0, 128), 7.0, A.is_equal)
@@ -584,52 +637,69 @@ def rank_program(g, core, T, topo):
         def offsets(hf):
             a0 = 128 * hf
             tt(S("mx", a0, a0 + 128), S("of", a0, a0 + 128), S("KT"), A.max)
-            ts(S("so", a0, a0 + 128), S("mx", a0, a0 + 128), -14336.0, A.add)
-        tests(1, (6, 0, 1, 2, 3, 4))
-        update(0, 5)
-        update(2, 5)
-        update(3, 5)
-        tests(1, (5,))
-        total(1)
+            ts(S("so", a0, a0 + 128), S("mx", a0, a0 + 128), float(SV - 16384), A.add)
+        tests(1, True)
+        passed_probes(2, 4, 6)
+        passed_probes(3, 5, 6)
+        passed_probes(0, 4, 6)
+        tests(1, False)
+        total(1, 5)
         passed(1)
         alive(1)
-        update(1, 5)
-        tests(0, (6, 0, 1, 2, 3, 4, 5))
+        passed_probes(1, 5, 6)
+        tests(0, True)
+        tests(0, False)
         number(1)
         passed(0)
         alive(0)
         offsets(1)
-        act(IND(S("SAf"), S("so", 128, 256)), S("Zf"), F.Silu)
+        act(IND(S("FW", SS, FX), S("so", 128, 256)), S("Zf"), F.Silu)
         number(0)
         offsets(0)
-        tt(S("nS"), S("sc", 31, 32), S("sc", 63, 64), A.add)
-        ts(S("dA"), S("sc", 31, 32), -1.0, A.mult, 2048.0, A.add)
-        ts(S("g2"), S("W3", 0, 256), S("nS"), A.is_gt, 8192.0, A.mult)
-        ts(S("g1"), S("W3", 0, 256), S("sc", 31, 32), A.is_gt, S("dA"), A.mult)
+        tt(S("nS"), S("m05"), S("sc", 31, 32), A.subtract)
+        ts(S("dA"), S("sc", 31, 32), -0.5, A.mult, 2048.0, A.add)
+        tt(S("nT"), S("nS"), S("sc", 63, 64), A.subtract)
+        act(S("g1"), S("W3", 0, 256), F.Sign, bias=S("nS"))
+        act(S("g2"), S("W3", 0, 256), F.Sign, bias=S("nT"))
+        act(S("g1"), S("g1"), F.Identity, bias=S("dA"), scale=S("dA"))
         mm(S("b4", 0, 256), S("identF"), S("W3", 0, 256), True, False)
         mm(S("b4", 0, 256), S("N16384"), S("Fl", 0, 256), False, False)
-        mm(S("b4", 0, 256), S("identF"), S("g2"), False, False)
+        mm(S("b4", 0, 256), S("I8192"), S("g2"), False, False)
         mm(S("b4", 0, 256), S("identF"), S("g1"), False, True)
-        cp(IND(S(cur, 0, SA), S("so", 0, 128)), S("Zp", 0, 2048))
-        act(S(cur, SA, SA + 1216), S("SAf", 2048, 3264), F.Relu, bias=-32.0005)
+        cp(IND(S("FW", 0, SS), S("so", 0, 128)), S("Zp", 0, 2048))
         tt(S("fo"), S("b4", 0, 256), S("VT"), A.min)
-        ts(S("fo16"), S("fo"), 16383.0, A.add)
-        ts(S(cur, SA + 1216, XO), S("SAf", 3264, 4096), MAGIC - 32.0, A.add, -MAGIC, A.add)
+        ts(S("fo16"), S("fo"), 24575.0, A.add)
 
         def place(b):
-            win = IND(S(cur, SV, XE), S("fo16", 32 * b, 32 * b + 32))
-            o = S(nxt, XO + 512 * b, XO + 512 * b + 512)
+            win = IND(S("FW", SV, FE), S("fo16", 32 * b, 32 * b + 32))
+            o = S(nxt, 512 * b, 512 * b + 512)
             if t < 2:
                 if b % 2 == 0:
                     cp(o, win)
                 else:
                     act(o, win, F.Copy)
+                return
+            if b % 2 == 0:
+                m = S("cmp", 512 * b, 512 * b + 512)
+                ts(m, win, -4079.986, A.add, 0.0, A.min)
+                ts(o, m, -0.0625, A.mult)
             else:
-                if b % 2 == 0:
-                    ts(o, win, -1.0, A.mult, 255.0, A.add)
-                else:
-                    act(o, win, F.Identity, bias=255.0, scale=-1.0)
-                op("sync", lambda: g.sync.dma_start(T.y[:, 512 * b:512 * b + 512], AP(o)), [o], [], "ys%d" % b, 16)
-        for b in range(8):
-            place(b)
+                act(o, win, F.Relu, bias=254.9991, scale=-0.0625)
+            op("sync", lambda: g.sync.dma_start(T.y[:, 512 * b:512 * b + 512], AP(o)), [o], [], "ys%d" % b, 16)
+        for k in range(4):
+            place(2 * k)
+            place(2 * k + 1)
+            if t < 2:
+                values(t + 1, 2 * k)
+                values(t + 1, 2 * k + 1)
+                if k:
+                    nonzero(t + 1, 2 * k - 2)
+                    nonzero(t + 1, 2 * k - 1)
+                    diagonal(2 * k - 2)
+                    diagonal(2 * k - 1)
+        if t < 2:
+            nonzero(t + 1, 6)
+            nonzero(t + 1, 7)
+            diagonal(6)
+            diagonal(7)
     emit()

import numpy as np
from concourse.bass import DstId, RemoteDMATransfer
from concourse.mybir import dt, AluOpType as A, AxisListType, ActivationFunctionType as F

XE, XC = 4096, 4128
SV, SS, FX, FE = 2048, 4096, 8192, 12288
SB = {
    "BW0": (XC, "bfloat16"), "BW1": (XC, "bfloat16"), "FW": (FE, "float32"), "Zp": (4096, "bfloat16"),
    "Zf": (2048, "float32"), "Pg": (1024, "bfloat16"), "Hs": (256, "bfloat16"), "Hl": (256, "bfloat16"),
    "c1n": (256, "bfloat16"), "c2n": (256, "bfloat16"), "c3n": (256, "bfloat16"),
    "c1p": (1024, "bfloat16"), "c2p": (1024, "bfloat16"), "c3p": (1024, "bfloat16"),
    "cmp": (4096, "bfloat16"), "G": (2048, "bfloat16"), "dg": (128, "float32"),
    "cown": (12, "float32"), "cl": (144, "float32"), "small": (16, "float32"), "lst": (160, "bfloat16"),
    "qi": (16, "int32"), "qf": (16, "float32"), "Qblk": (128, "bfloat16"), "nQ4": (512, "bfloat16"), "kapT": (512, "float32"),
    "pi": (1, "int32"), "p16i": (1, "int32"), "pgi": (1, "int32"), "pif": (1, "float32"), "p16f": (1, "float32"),
    "pgf": (1, "float32"), "e15": (1, "float32"), "p37": (1, "float32"), "ci": (144, "int32"), "cg": (128, "int32"),
    "Bones": (128, "bfloat16"), "BonesF": (128, "float32"), "ident": (128, "bfloat16"), "identF": (128, "float32"),
    "nident": (128, "bfloat16"), "I3856": (128, "bfloat16"), "I16384": (128, "bfloat16"), "I8192": (128, "bfloat16"),
    "N16384": (128, "bfloat16"), "EM1": (144, "bfloat16"), "I16": (128, "bfloat16"),
    "EM241": (144, "bfloat16"), "EM120": (144, "bfloat16"), "E": (144, "bfloat16"), "M16f": (16, "float32"),
    "mask16": (16, "float32"), "base": (16, "float32"), "obig": (16, "float32"), "rown": (48, "float32"),
    "Dm": (128, "bfloat16"), "Ds": (128, "bfloat16"), "dtmp": (128, "bfloat16"),
    "B4080": (128, "bfloat16"), "c4080": (128, "bfloat16"), "Ji": (602, "int32"), "Jm": (602, "int32"), "JF": (602, "float32"),
    "IF": (1024, "float32"), "IU": (1024, "uint16"), "JTi": (384, "int32"), "JTk": (384, "int32"), "JTm": (384, "int32"),
    "JT": (384, "float32"), "VTi": (256, "int32"), "VT": (256, "float32"), "KT": (128, "float32"),
    "onesF": (256, "float32"), "W2": (48, "float32"), "W3": (528, "float32"),
    "mn": (1, "float32"), "oh": (16, "float32"), "cq": (16, "float32"), "csel": (1, "float32"),
    "csb": (1, "bfloat16"), "kaps": (1, "float32"), "kap2": (1, "float32"), "Fl": (512, "bfloat16"), "T2b": (32, "bfloat16"),
    "I3": (512, "float32"), "I2": (32, "float32"), "bt": (32, "float32"), "bnd": (8, "float32"),
    "oAn": (16, "uint16"), "oQn": (16, "uint16"), "oPn": (16, "uint16"), "oAp": (64, "uint16"), "oQp": (64, "uint16"),
    "oPp": (64, "uint16"), "A17": (64, "float32"), "AF": (64, "float32"),
    "t32": (256, "int32"), "vi": (256, "int32"), "off": (256, "uint16"), "Tf5": (256, "float32"), "eq": (256, "bfloat16"),
    "NZ": (1792, "bfloat16"), "shr": (48, "float32"), "AL": (256, "bfloat16"), "sc": (64, "float32"), "pb": (64, "float32"),
    "of": (256, "float32"), "mx": (256, "float32"), "so": (256, "uint16"),
    "g1": (256, "float32"), "g2": (256, "bfloat16"), "fo": (256, "float32"), "fo16": (256, "uint16"),
}
PART = {"lAn": ("lst", 0, 16), "lQn": ("lst", 16, 16), "lAp": ("lst", 32, 64), "lQp": ("lst", 96, 64),
        "m05": ("small", 0, 1), "nT": ("small", 4, 1), "nS": ("small", 8, 1), "dA": ("small", 12, 1)}
for _t in range(3):
    PART["cown%d" % _t] = ("cown", 4 * _t, 1)
    PART["rown%d" % _t] = ("rown", 16 * _t, 16)
    PART["cl%d" % _t] = ("cl", 48 * _t, 48)
SCRATCH = {n: ("sbuf", [128, -(-c // 16) * 16], d) for n, (c, d) in SB.items()}
for _b in range(8):
    SCRATCH["b%d" % _b] = ("psum", [128, 512], "float32")
NX = 8
QSEM = {"tensor": "sT", "vector": "sV", "scalar": "sS", "g": "sG"}
SEMAPHORES = (["sT", "sV", "sS", "sG", "qld"] + ["xl%d" % i for i in range(NX)] + ["ys%d" % i for i in range(8)]
              + ["%s%d" % (s, t) for s in ("cs", "gs", "lc", "lg", "fx", "fz") for t in range(3)])
XS = (1, 2, 3)
BIG = 1048576.0
LOOP = "a2 b2 o2 a0 g2 e2 b0 a3 x2 b3 y2 o0 o3 c0 a1 g3 e0 u2 v2 b1 e3 s y3 v3 x3 o1 t2 e1 u3 t0 c1 t3 t1"
CE = 4


def make_queue(g, T):
    ops, hist = [], {}
    eng = {"tensor": g.tensor, "vector": g.vector, "scalar": g.scalar, "sync": g.sync, "g": g}

    def op(q, fn, reads, writes, sem=None, val=0, remote=False):
        me = len(ops)
        rec = {"q": q, "fn": fn, "deps": set(), "sem": sem, "val": val, "need": False, "m": [], "remote": remote}
        acc = []
        for w in writes:
            if w[0] == "IND":
                acc += [(w[1], True), (w[2], False)]
            else:
                acc.append((w, True))
        for r in reads:
            if r[0] == "IND":
                acc += [(r[1], False), (r[2], False)]
            else:
                acc.append((r, False))

        def mine(o):
            return o["q"] == q and o["sem"] is None
        for (n, a, b, _ap), isw in acc:
            ps = n[0] == "b" and len(n) == 2
            for (oa, ob, o, ow) in hist.setdefault(n, []):
                if o == me:
                    continue
                hit = oa < b and a < ob
                if mine(ops[o]):
                    need = hit and ow and not (ps and q == "tensor")
                else:
                    need = ps or (hit and (ow or isw))
                if need:
                    rec["deps"].add(o)
        ops.append(rec)
        for (n, a, b, _ap), isw in acc:
            ps = n[0] == "b" and len(n) == 2
            keep = []
            for e in hist[n]:
                inside = a <= e[0] and e[1] <= b
                if e[2] != me and ((inside and isw) or (inside and not e[3] and mine(ops[e[2]]))
                                   or (ps and not mine(ops[e[2]]) and not e[3])):
                    continue
                keep.append(e)
            keep.append((a, b, me, isw))
            hist[n] = keep

    def emit():
        for r in ops:
            for d in r["deps"]:
                ops[d]["need"] = True
        cnt = {q: 0 for q in QSEM}
        know = {q: {} for q in eng}
        for r in ops:
            q = r["q"]
            if q is None:
                r["clock"] = {r["sem"]: r["val"], "own": r["sem"]}
                continue
            k = know[q]
            todo = {}
            for d in sorted(r["deps"], reverse=True):
                o = ops[d]
                s, v = (o["sem"], o["val"]) if o["sem"] is not None else (QSEM[o["q"]], o["at"])
                if k.get(s, 0) < v and todo.get(s, 0) < v:
                    todo[s] = v
                    r["m"].append(o["clock"])
            for s in sorted(todo):
                if not any(c["own"] != s and c.get(s, 0) >= todo[s] for c in r["m"]):
                    eng[q].wait_ge(T.sem[s], int(todo[s]))
            for c in r["m"]:
                for s, v in c.items():
                    if s != "own" and k.get(s, 0) < v:
                        k[s] = v
            ins = r["fn"]()
            if r["sem"] is not None:
                c = dict(k)
                c[r["sem"]] = r["val"]
                c["own"] = r["sem"]
                if not r["remote"]:
                    ins.then_inc(T.sem[r["sem"]], r["val"])
            else:
                s = QSEM[q]
                c = dict(k)
                c["own"] = s
                if r["need"]:
                    cnt[q] += 1
                    ins.then_inc(T.sem[s], 1)
                    c[s] = cnt[q]
                    r["at"] = cnt[q]
            r["clock"] = c
        for q, n in cnt.items():
            if n:
                g.wait_ge(T.sem[QSEM[q]], n)
        for r in ops:
            if r["sem"] is not None and r["sem"][:2] in ("ys", "lc", "lg"):
                g.wait_ge(T.sem[r["sem"]], r["val"])

    return op, emit


def rank_program(g, core, T, topo):
    rank = T.rank_of(core)
    if rank is None:
        return
    op, emit = make_queue(g, T)

    def S(n, a=0, b=None, st=1):
        n, o, w = PART.get(n, (n, 0, SB[n][0] if n in SB else 512))
        a, b = a + o, (w if b is None else b) + o
        return (n, a, b, T[n][:, a:b] if st == 1 else T[n][:, a:b:st])

    def IND(w, o):
        return ("IND", w, o)

    def AP(x):
        return x[1][3].indirect(x[2][3]) if x[0] == "IND" else x[3]

    def num(x):
        return isinstance(x, (int, float))

    def cp(out, in_):
        op("vector", lambda: g.vector.tensor_copy(AP(out), AP(in_)), [in_], [out])

    def tt(out, a, b, o):
        op("vector", lambda: g.vector.tensor_tensor(AP(out), AP(a), AP(b), o), [a, b], [out])

    def ts(out, a, s1, o0, s2=None, o1=None):
        cols = [x for x in (s1, s2) if x is not None and not num(x)]
        u1 = s1 if num(s1) else AP(s1)
        if o1 is None:
            op("vector", lambda: g.vector.tensor_scalar(AP(out), AP(a), u1, None, o0), [a] + cols, [out])
        else:
            u2 = s2 if num(s2) else AP(s2)
            op("vector", lambda: g.vector.tensor_scalar(AP(out), AP(a), u1, u2, o0, o1), [a] + cols, [out])

    def red(out, a, o):
        op("vector", lambda: g.vector.tensor_reduce(AP(out), AP(a), AxisListType.X, o), [a], [out])

    def scan(out, a, n):
        one = S("onesF", 0, n)
        op("vector", lambda: g.vector.tensor_tensor_scan(AP(out), AP(one), AP(a), 0.0, A.mult, A.add), [one, a], [out])

    def fill(out, c):
        op("vector", lambda: g.vector.memset(AP(out), c), [], [out])

    def act(out, a, f, bias=0.0, scale=1.0):
        if f == F.Silu:
            op("scalar", lambda: g.scalar.activation(AP(out), AP(a), f), [a], [out])
        else:
            cols = [x for x in (bias, scale) if not num(x)]
            ub, us = bias if num(bias) else AP(bias), scale if num(scale) else AP(scale)
            op("scalar", lambda: g.scalar.activation(AP(out), AP(a), f, bias=ub, scale=us), [a] + cols, [out])

    def mm(out, l, r, start, stop):
        op("tensor", lambda: g.tensor.matmul(AP(out), AP(l), AP(r), start, stop), [l, r], [out])

    def spread(bank, c0, n, emat, src, s0, start, stop):
        for p in range(16):
            mm(S(bank, c0, c0 + n), S(emat, 15 - p, 143 - p), S(src, s0 + p, s0 + 16 * n, 16), start and p == 0, stop and p == 15)

    def iota(out, pattern, base=0, cm=0, fl=False):
        if fl:
            op("g", lambda: g.iota(AP(out), pattern, base, cm, allow_small_or_imprecise_dtypes=True), [], [out])
        else:
            op("g", lambda: g.iota(AP(out), pattern, base, cm), [], [out])

    def cast_in(out, in_ap, reads, sem):
        op("g", lambda: g.dma_start(AP(out), in_ap), reads, [out], sem, 16)

    op("sync", lambda: g.sync.dma_start(T.qi[:, 0:16], T.q[:]), [], [S("qi")], "qld", 16)
    w = 4096 // NX

    def load(i, q):
        o = S("BW1", w * i, w * i + w)
        op(q, lambda: (g.sync if q == "sync" else g.scalar).dma_start(AP(o), T.x[:, w * i:w * i + w]), [], [o], "xl%d" % i, 16)
    for i in range(NX):
        load(i, "sync" if i % 2 else "scalar")
    iota(S("pi"), [[1, 1]], 0, 1)
    iota(S("ci"), [[1, 144]])
    iota(S("Ji"), [[37, 602]])
    iota(S("IF"), [[1, 1024]], 0, 0, True)
    iota(S("JTi"), [[1, 3], [64, 4], [592, 32]])
    iota(S("VTi"), [[16, 256]], FX - SV)
    iota(S("KT"), [[16, 128]], 16384 - SV, 0, True)
    ts(S("pgi"), S("pi"), 4, A.arith_shift_right)
    ts(S("cg"), S("ci", 0, 128), 4, A.arith_shift_right)
    ts(S("p16i"), S("pi"), 15, A.bitwise_and)
    cp(S("pgf"), S("pgi"))
    cp(S("pif"), S("pi"))
    cp(S("p16f"), S("p16i"))
    ts(S("BonesF"), S("cg"), S("pgf"), A.is_equal)
    ts(S("identF"), S("ci", 0, 128), S("pif"), A.is_equal)
    for k in range(8):
        ts(S("Qblk", 16 * k, 16 * k + 16), S("qi"), S("BonesF", 16 * k, 16 * k + 1), A.mult)
    ts(S("M16f"), S("ci", 0, 16), S("p16f"), A.is_equal, 16.0, A.mult)
    cp(S("base"), S("ci", 0, 16))
    tt(S("e15"), S("pif"), S("p16f"), A.subtract)

    def consts_a():
        ts(S("e15"), S("e15"), 15.0, A.add)
        cp(S("qf"), S("qi"))
        ts(S("dtmp"), S("ci", 0, 128), S("pif"), A.is_lt, -1.0, A.mult)
        ts(S("EM1"), S("ci"), S("e15"), A.is_equal)
        act(S("Bones"), S("BonesF"), F.Copy)
        act(S("B4080"), S("BonesF"), F.Copy, scale=4080.0)
        act(S("ident"), S("identF"), F.Copy)
        tt(S("Dm"), S("dtmp"), S("BonesF"), A.mult)
        act(S("I16"), S("identF"), F.Copy, scale=16.0)
        for b in range(8):
            o, i = S("BW0", 512 * b, 512 * b + 512), S("BW1", 512 * b, 512 * b + 512)
            if b in (2, 5, 7):
                act(o, i, F.Identity, bias=4080.0, scale=-16.0)
            else:
                ts(o, i, -16.0, A.mult, 4080.0, A.add)
        fill(S("BW0", XE, XC), 0.0)
        fill(S("BW1", XE, XC), 0.0)
        ts(S("mask16"), S("M16f"), 0.0625, A.mult)
        fill(S("onesF"), 1.0)
        for a, b in ((16, 24), (40, 48)):
            fill(S("W2", a, b), 1000000.0)
        for a, b in ((256, 264), (520, 528)):
            fill(S("W3", a, b), 1000000.0)

    def consts_b():
        for n, s in (("EM241", 241.0), ("EM120", 120.5)):
            act(S(n), S("EM1"), F.Copy, scale=s)
        for n, s in (("nident", -1.0), ("I3856", 3856.0), ("I16384", 16384.0), ("I8192", 8192.0), ("N16384", -16384.0)):
            act(S(n), S("identF"), F.Copy, scale=s)
        for k in range(3):
            act(S("FW", SV + 2048 * k, SV + 2048 * k + 2048), S("BW1", 0, 2048), F.Copy)
        ts(S("Jm"), S("Ji"), 255, A.bitwise_and)
        fill(S("m05"), -0.5)
        ts(S("p37"), S("p16f"), 37.0, A.mult)
        cp(S("JF"), S("Jm"))

    def consts_c():
        ts(S("JTk"), S("JTi"), S("p37"), A.add)
        ts(S("JTm"), S("JTk"), 255, A.bitwise_and)

    def consts_f():
        tt(S("Ds"), S("Dm"), S("identF"), A.subtract)
        ts(S("VT"), S("VTi"), S("p16f"), A.add, -24575.0, A.add)
        ts(S("KT"), S("KT"), S("p16f"), A.add)

    def consts_d():
        cp(S("IU"), S("IF"))

    def consts_e():
        for k in range(4):
            act(S("nQ4", 128 * k, 128 * k + 128), S("Qblk"), F.Copy, scale=-1.0)
        fill(S("c4080"), 4080.0)
        mm(S("b5"), S("c4080"), S("nQ4"), True, True)
        act(S("kapT"), S("b5"), F.Copy, scale=-1.0)

    peers = [r for r in range(len(T.cores)) if r != rank]
    peers.sort(key=lambda r: len(topo.engines(core, T.cores[r])))
    used, plan = [], []
    for r in peers:
        es = [e for e in topo.engines(core, T.cores[r]) if e not in used][:CE]
        used += es
        plan.append((r, sum(1 << e for e in es)))

    def send_counts(t):
        def f():
            tr = []
            for r, m in plan:
                rid, pid, _s = topo.addr(T.cores[r])
                c = [k for k in range(len(T.cores)) if k != r].index(rank)
                tr.append(RemoteDMATransfer(dst_ids=[DstId(rid=rid, pnc=pid)], dma_engine_mask=m, remote_sem=T.sem["cs%d" % t],
                                            src=AP(S("rown%d" % t)), dst=AP(S("cl%d" % t, 16 * c, 16 * c + 16))))
            return g.remote_dma_fused(tr, local_sem=T.sem["lc%d" % t])
        op("g", f, [S("rown%d" % t)], [], "lc%d" % t, CE * len(peers), True)
        op(None, None, [], [S("cl%d" % t)], "cs%d" % t, CE * len(peers))

    def send_guests(t):
        dst = T.cores[rank ^ XS[t]]
        es = topo.engines(core, dst)[:8]

        def f():
            rid, pid, _s = topo.addr(dst)
            return g.remote_dma(T.Hl[:, 0:256], T.Hs[:, 0:256], T.sem["gs%d" % t], T.sem["lg%d" % t], pid, rid, sum(1 << e for e in es))
        op("g", f, [S("Hs")], [], "lg%d" % t, len(es), True)

    def guests_come(t):
        src = T.cores[rank ^ XS[t]]
        op(None, None, [], [S("Hl")], "gs%d" % t, len(topo.engines(src, core)[:8]))

    def values(t, b):
        xs, bank = "BW1" if t < 2 else "BW0", "b%d" % (b % 7)
        shift = t > 0 and b % 2 == 1
        if shift:
            mm(S(bank), S("c4080"), S("nQ4"), True, False)
        for k in range(4):
            mm(S(bank, 128 * k, 128 * k + 128), S(xs, 512 * b + 128 * k, 512 * b + 128 * k + 128), S("Qblk"), not shift,
               not shift or k == 3)

    def nonzero(t, b):
        bank, o = S("b%d" % (b % 7)), S("cmp", 512 * b, 512 * b + 512)
        if b % 2 == 1:
            act(o, bank, F.Sign)
        elif t == 0:
            ts(o, bank, 0.0, A.not_equal)
        else:
            tt(o, bank, S("kapT"), A.not_equal)

    def diagonal(b):
        for k in range(4):
            c = S("cmp", 512 * b + 128 * k, 512 * b + 128 * k + 128)
            mm(S("b7", 0, 128), c, c, b == 0 and k == 0, b == 7 and k == 3)

    for b in range(4):
        values(0, b)
    for b in range(8):
        nonzero(0, b)
        diagonal(b)
        if b < 4:
            values(0, b + 4)
    for t in range(3):
        cur, nxt = ("BW0", "BW1") if t % 2 == 0 else ("BW1", "BW0")
        X = S(cur, 0, XC)
        cown, rown = S("cown%d" % t), S("rown%d" % t)
        tt(S("dg"), S("b7", 0, 128), S("identF"), A.mult)
        red(cown, S("dg"), A.add)
        ts(rown, S("M16f"), cown, A.mult)
        send_counts(t)
        mm(S("b0", 0, 16), S("identF"), S("base"), True, False)
        mm(S("b0", 0, 16), S("BonesF"), rown, False, False)
        if t == 0:
            consts_a()
        if t == 1:
            consts_d()
        for k in range(3):
            mm(S("b0", 0, 16), S("BonesF"), S("cl%d" % t, 16 * k, 16 * k + 16), False, k == 2)
        red(S("mn"), S("b0", 0, 16), A.min)
        ts(S("oh"), S("b0", 0, 16), S("mn"), A.is_equal)
        tt(S("cq"), S("oh"), S("qf"), A.mult)
        red(S("csel"), S("cq"), A.add)
        ts(S("E"), S("EM1"), S("csel"), A.mult)
        cp(S("csb"), S("csel"))
        mm(S("b1", 0, 1), S("B4080"), S("csb"), True, True)
        spread("b2", 0, 256, "E", cur, 0, True, True)
        cp(S("kaps"), S("b1", 0, 1))
        ts(S("obig"), S("oh"), BIG, A.mult)
        ts(S("kap2"), S("kaps"), 2.0, A.mult)
        tt(S("base"), S("base"), S("obig"), A.add)
        if t == 0:
            consts_b()
        ts(S("Fl", 0, 256), S("b2", 0, 256), S("kaps"), A.is_gt)
        ts(S("Fl", 256, 512), S("b2", 0, 256), S("kaps"), A.is_lt)
        for p in range(16):
            mm(S("b3", 0, 32), S("EM1", 15 - p, 143 - p), S("Fl", p, 512, 16), p == 0, p == 15)
        mm(S("b4"), S("Bones"), S("Fl"), True, True)
        mm(S("b5"), S("Dm"), S("Fl"), True, True)
        if t == 0:
            consts_c()
        cp(S("T2b"), S("b3", 0, 32))
        mm(S("b6", 0, 32), S("Bones"), S("T2b"), True, True)
        mm(S("b6", 32, 64), S("Dm"), S("T2b"), True, True)
        scan(S("I3", 0, 256), S("b4", 0, 256), 256)
        scan(S("I2", 0, 16), S("b6", 0, 16), 16)
        scan(S("I2", 16, 32), S("b6", 16, 32), 16)
        tt(S("bt", 0, 16), S("I2", 0, 16), S("mask16"), A.mult)
        tt(S("bt", 16, 32), S("I2", 16, 32), S("mask16"), A.mult)
        red(S("bnd", 0, 1), S("bt", 0, 16), A.add)
        red(S("bnd", 4, 5), S("bt", 16, 32), A.add)
        J = S("JF", 173 * t, 173 * t + 256)
        ts(S("c1n"), J, S("bnd", 0, 1), A.is_ge)
        spread("b7", 0, 16, "EM1", "c1n", 0, True, True)
        ts(S("c1p"), S("IF" if t == 0 else "IU"), S("bnd", 4, 5), A.is_ge)
        spread("b1", 0, 64, "EM1", "c1p", 0, True, True)
        tt(S("W2", 0, 16), S("I2", 0, 16), S("b6", 32, 48), A.add)
        tt(S("W2", 24, 40), S("I2", 16, 32), S("b6", 48, 64), A.add)
        cp(S("oAn"), S("b7", 0, 16))
        act(S("lAn"), S("b7", 0, 16), F.Copy)
        tt(S("c2n"), IND(S("W2", 0, 24), S("oAn")), J, A.is_le)
        mm(S("b0", 0, 16), S("I16"), S("lAn"), True, False)
        spread("b0", 0, 16, "EM1", "c2n", 0, False, True)
        tt(S("W3", 0, 256), S("I3", 0, 256), S("b5", 0, 256), A.add)
        cp(S("oAp"), S("b1", 0, 64))
        act(S("lAp"), S("b1", 0, 64), F.Copy)
        qb, pbk = ("b6", "b2"), ("b7", "b1")

        def find2(h):
            o, k = (512 * h, 512 * h + 512), (32 * h, 32 * h + 32)
            tt(S("c2p", *o), IND(S("W2", 24, 48), S("oAp", *k)), S("IF", *o), A.is_le)
            mm(S(qb[h], 0, 32), S("I16"), S("lAp", *k), True, False)
            spread(qb[h], 0, 32, "EM1", "c2p", 512 * h, False, True)

        def find3(h):
            o, k = (512 * h, 512 * h + 512), (32 * h, 32 * h + 32)
            cp(S("oQp", *k), S(qb[h], 0, 32))
            act(S("lQp", *k), S(qb[h], 0, 32), F.Copy)
            tt(S("c3p", *o), IND(S("W3", 264, 528), S("oQp", *k)), S("IF", *o), A.is_le)
            mm(S(pbk[h], 0, 32), S("I16"), S("lQp", *k), True, False)
            spread(pbk[h], 0, 32, "EM1", "c3p", 512 * h, False, True)

        def start(h):
            k = (32 * h, 32 * h + 32)
            cp(S("oPp", *k), S(pbk[h], 0, 32))
            ts(S("A17", *k), S(pbk[h], 0, 32), 17.0, A.mult)
            cp(S("AF", *k), S(pbk[h], 0, 32))
            act(S("Pg", 512 * h, 512 * h + 512), IND(X, S("oPp", *k)), F.Copy)
            for ww in range(4):
                o = 128 * h + 32 * ww
                tt(S("t32", o, o + 32), S("A17", *k), S("JT", 128 * t + 32 * ww, 128 * t + 32 * ww + 32), A.add)
            o = (128 * h, 128 * h + 128)
            ts(S("vi", *o), S("t32", *o), 4095, A.bitwise_and)
            cp(S("off", *o), S("vi", *o))

        def own_places(h):
            for c in (2 * h, 2 * h + 1):
                for k in range(2):
                    mm(S("b%d" % c, 384 + 32 * k, 416 + 32 * k), S("identF"), S("AF", 32 * h, 32 * h + 32), True, True)
        cp(S("oQn"), S("b0", 0, 16))
        act(S("lQn"), S("b0", 0, 16), F.Copy)
        tt(S("c3n"), IND(S("W3", 0, 264), S("oQn")), J, A.is_le)
        mm(S("b3", 0, 16), S("I16"), S("lQn"), True, False)
        spread("b3", 0, 16, "EM1", "c3n", 0, False, True)
        scan(S("I3", 256, 512), S("b4", 256, 512), 256)
        find2(0)
        tt(S("W3", 264, 520), S("I3", 256, 512), S("b5", 256, 512), A.add)
        cp(S("oPn"), S("b3", 0, 16))
        act(S("Hs"), IND(X, S("oPn")), F.Copy)
        send_guests(t)
        find2(1)
        find3(0)
        find3(1)
        if t == 0:
            ts(S("JT"), S("JTm"), 5.0, A.mult)
        start(0)
        own_places(0)
        start(1)
        own_places(1)
        if t == 0:
            consts_f()
            consts_e()

        def gather_s(c):
            act(S("G", 1024 * (c - 2), 1024 * (c - 2) + 1024), IND(X, S("off", 64 * c, 64 * c + 64)), F.Copy)

        def equal(c):
            h = (64 * c, 64 * c + 64)
            ts(S("Tf5", *h), S("vi", *h), 5.0, A.mult, 1.0 if c < 2 else 1929.0, A.add)
            tt(S("eq", *h), S("vi", *h), S("b%d" % c, 384, 448), A.is_equal)
        gather_s(2)
        gather_s(3)
        guests_come(t)
        cast_in(S("FW", FX, FE), T[cur][:, 0:4096], [S(cur, 0, XE), S("Hl")], "fx%d" % t)
        ub = {0: 4, 1: 6, 2: 6, 3: 4}

        def sums(c):
            for k in range(2):
                ww = 2 * (c % 2) + k
                b = "b%d" % (ub[c] + k)
                mm(S(b), S("ident"), S("Pg", 512 * (c // 2), 512 * (c // 2) + 512), True, False)
                for o in (0, 256):
                    mm(S(b, o, o + 256 - 64 * ww), S("ident"), S("Hl", 64 * ww, 256), False, o == 256 and ww == 0)
                    if ww:
                        mm(S(b, o + 256 - 64 * ww, o + 256), S("ident"), S("Hl", 0, 64 * ww), False, o == 256)

        def children(c):
            for k in range(2):
                b = S("b%d" % (ub[c] + k))
                o = S("Zp", 1024 * c + 512 * k, 1024 * c + 512 * k + 512)
                if c == 3:
                    act(o, b, F.Relu, bias=-4080.0)
                else:
                    ts(o, b, -4080.0, A.add, 0.0, A.max)

        def diff(c, ks=(0, 1)):
            for k in ks:
                b = "b%d" % (2 * c + k)
                o = 1024 * (c - 2) + 512 * k
                mm(S(b), S("ident"), S("Zp", 1024 * c + 512 * k, 1024 * c + 512 * k + 512), True, False)
                mm(S(b), S("nident"), S("G", o, o + 512), False, True)

        def sign(c, ks=(0, 1)):
            for k in ks:
                o = 1024 * c + 512 * k
                act(S("cmp", o, o + 512), S("b%d" % (2 * c + k)), F.Sign, bias=-0.5)

        def compare(c):
            tt(S("cmp", 1024 * c, 1024 * c + 1024), IND(X, S("off", 64 * c, 64 * c + 64)), S("Zp", 1024 * c, 1024 * c + 1024), A.is_lt)

        def total(c, n):
            b = "b%d" % c
            mm(S(b, 64 * n, 64 * n + 64), S("I3856"), S("eq", 64 * c, 64 * c + 64), True, False)
            spread(b, 64 * n, 64, "EM241" if c < 2 else "EM120", "cmp", 1024 * c, False, True)

        def update(c, n):
            h = (64 * c, 64 * c + 64)
            tt(S("t32", *h), S("b%d" % c, 64 * n, 64 * n + 64), S("Tf5", *h), A.add)

        def wrap(c):
            h = (64 * c, 64 * c + 64)
            ts(S("vi", *h), S("t32", *h), 4095, A.bitwise_and)

        def offs(c):
            h = (64 * c, 64 * c + 64)
            cp(S("off", *h), S("vi", *h))

        def passed_probes(c, n0, n1):
            ts(S("NZ", 384 * c + 64 * n0, 384 * c + 64 * n1), S("b%d" % c, 64 * n0, 64 * n1), 0.0 if c < 2 else -1928.0, A.not_equal)

        def sum_ok(hf):
            for ww in range(4):
                o = 1536 + 128 * hf + 32 * ww
                tt(S("NZ", o, o + 32), S("b1", 448 + 32 * hf, 480 + 32 * hf), S("shr", 4 * ww, 4 * ww + 32), A.is_le)

        sums(0)
        sums(2)
        children(0)
        for c in (0, 2, 1, 3):
            equal(c)
        sums(3)
        children(2)
        children(3)
        sums(1)
        diff(2)
        compare(0)
        children(1)
        diff(3)
        sign(2)
        total(2, 0)
        total(0, 0)
        compare(1)
        sign(3)
        total(3, 0)
        total(1, 0)
        cast_in(S("Zf"), T.Zp[:, 2048:4096], [S("Zp", 2048, 4096)], "fz%d" % t)
        do = {"a": update, "b": lambda c, n: wrap(c), "o": lambda c, n: offs(c), "e": lambda c, n: equal(c),
              "g": lambda c, n: gather_s(c), "c": lambda c, n: compare(c), "t": lambda c, n: total(c, n + 1),
              "x": lambda c, n: diff(c, (0,)), "y": lambda c, n: diff(c, (1,)),
              "u": lambda c, n: sign(c, (0,)), "v": lambda c, n: sign(c, (1,))}
        for n in range(5):
            for k in LOOP.split():
                if k == "s":
                    if n == 0:
                        spread("b1", 448, 64, "E", "Pg", 0, True, True)
                        spread("b0", 448, 16, "E", "Hl", 0, True, True)
                        for m in range(3):
                            ts(S("shr", 16 * m, 16 * m + 16), S("b0", 448, 464), -1.0, A.mult, S("kap2"), A.add)
                    elif n < 3:
                        sum_ok(n - 1)
                    else:
                        for c in ((0, 2), (1, 3))[n - 3]:
                            passed_probes(c, 0, n + 1)
                elif (k, n) != ("t1", 4):
                    do[k[0]](int(k[1]), n)

        def tests(hf, early):
            b = "b%d" % (4 + hf)
            if early:
                mm(S(b, 0, 128), S("ident"), S("NZ", 1536 + 128 * hf, 1664 + 128 * hf), True, False)
            for n in (range(4) if early else (4, 5)):
                for k in range(2):
                    o = 384 * (2 * hf + k) + 64 * n
                    mm(S(b, 64 * k, 64 * k + 64), S("ident"), S("NZ", o, o + 64), False, n == 5 and k == 1)

        def passed(hf):
            ts(S("AL", 128 * hf, 128 * hf + 128), S("b%d" % (4 + hf), 0, 128), 7.0, A.is_equal)

        def alive(hf):
            bs, bx, a0 = "b%d" % (2 * hf), "b%d" % (2 * hf + 1), 128 * hf
            al = [S("AL", a0 + 32 * ww, a0 + 32 * ww + 32) for ww in range(4)]
            for ww in range(4):
                mm(S(bx, 0, 32), S("Bones"), al[ww], ww == 0, ww == 3)
            for ww in range(4):
                mm(S(bx, 32, 64), S("Ds"), al[ww], ww == 0, ww == 3)
            for ww in range(4):
                mm(S(bs, 32 * ww, 32 * ww + 32), S("I16384"), al[ww], True, ww == 0)
                for w2 in range(ww):
                    mm(S(bs, 32 * ww, 32 * ww + 32), S("ident"), al[w2], False, w2 == ww - 1)

        def number(hf):
            bs, bx, a0 = "b%d" % (2 * hf), "b%d" % (2 * hf + 1), 128 * hf
            sc, pb = S("sc", 32 * hf, 32 * hf + 32), S("pb", 32 * hf, 32 * hf + 32)
            scan(sc, S(bx, 0, 32), 32)
            tt(pb, sc, S(bx, 32, 64), A.add)
            for ww in range(4):
                tt(S("of", a0 + 32 * ww, a0 + 32 * ww + 32), S(bs, 32 * ww, 32 * ww + 32), pb, A.add)

        def offsets(hf):
            a0 = 128 * hf
            tt(S("mx", a0, a0 + 128), S("of", a0, a0 + 128), S("KT"), A.max)
            ts(S("so", a0, a0 + 128), S("mx", a0, a0 + 128), float(SV - 16384), A.add)
        tests(1, True)
        passed_probes(2, 4, 6)
        passed_probes(3, 5, 6)
        passed_probes(0, 4, 6)
        tests(1, False)
        total(1, 5)
        passed(1)
        alive(1)
        passed_probes(1, 5, 6)
        tests(0, True)
        tests(0, False)
        number(1)
        passed(0)
        alive(0)
        offsets(1)
        act(IND(S("FW", SS, FX), S("so", 128, 256)), S("Zf"), F.Silu)
        number(0)
        offsets(0)
        tt(S("nS"), S("m05"), S("sc", 31, 32), A.subtract)
        ts(S("dA"), S("sc", 31, 32), -0.5, A.mult, 2048.0, A.add)
        tt(S("nT"), S("nS"), S("sc", 63, 64), A.subtract)
        act(S("g1"), S("W3", 0, 256), F.Sign, bias=S("nS"))
        act(S("g2"), S("W3", 0, 256), F.Sign, bias=S("nT"))
        act(S("g1"), S("g1"), F.Identity, bias=S("dA"), scale=S("dA"))
        mm(S("b4", 0, 256), S("identF"), S("W3", 0, 256), True, False)
        mm(S("b4", 0, 256), S("N16384"), S("Fl", 0, 256), False, False)
        mm(S("b4", 0, 256), S("I8192"), S("g2"), False, False)
        mm(S("b4", 0, 256), S("identF"), S("g1"), False, True)
        cp(IND(S("FW", 0, SS), S("so", 0, 128)), S("Zp", 0, 2048))
        tt(S("fo"), S("b4", 0, 256), S("VT"), A.min)
        ts(S("fo16"), S("fo"), 24575.0, A.add)

        def place(b):
            win = IND(S("FW", SV, FE), S("fo16", 32 * b, 32 * b + 32))
            o = S(nxt, 512 * b, 512 * b + 512)
            if t < 2:
                if b % 2 == 0:
                    cp(o, win)
                else:
                    act(o, win, F.Copy)
                return
            if b % 2 == 0:
                m = S("cmp", 512 * b, 512 * b + 512)
                ts(m, win, -4079.986, A.add, 0.0, A.min)
                ts(o, m, -0.0625, A.mult)
            else:
                act(o, win, F.Relu, bias=254.9991, scale=-0.0625)
            op("sync", lambda: g.sync.dma_start(T.y[:, 512 * b:512 * b + 512], AP(o)), [o], [], "ys%d" % b, 16)
        for k in range(4):
            place(2 * k)
            place(2 * k + 1)
            if t < 2:
                values(t + 1, 2 * k)
                values(t + 1, 2 * k + 1)
                if k:
                    nonzero(t + 1, 2 * k - 2)
                    nonzero(t + 1, 2 * k - 1)
                    diagonal(2 * k - 2)
                    diagonal(2 * k - 1)
        if t < 2:
            nonzero(t + 1, 6)
            nonzero(t + 1, 7)
            diagonal(6)
            diagonal(7)
    emit()
